import numpy as np, ml_dtypes
CORES = [16,23,24,31,64,71]
N = 6
R, KR, T = 4096, 32768, 1024
CAPP = 256
def entries(a): return a.T.reshape(-1)
def pack(v, P): return np.ascontiguousarray(np.asarray(v, np.int32).reshape(-1, P).T)
def owners(rng, n, cap):
    return np.stack([rng.permutation(np.repeat(np.arange(N), cap))[:n] for r in range(N)])
def lists(rng, how):
    K = rng.permutation(N * KR)[:N * R]
    G = R * owners(rng, T, CAPP) + rng.integers(0, R, (N, T))
    if how == "uniform": G[:, :T // 8] = -1
    if how == "alike": O = np.stack([np.repeat(rng.permutation(N)[:T // CAPP], CAPP) for r in range(N)]); G = R * O + rng.integers(0, R, N)[O]
    if how == "edge":
        en = np.concatenate([KR * np.arange(N), KR * np.arange(N) + KR - 1]); ep = np.concatenate([R * np.arange(N), R * np.arange(N) + R - 1])
        K = rng.permutation(np.setdiff1d(np.arange(N * KR), en))[:N * R]; K[ep] = rng.permutation(en)
        G = np.concatenate([np.tile(ep, (N, 1)), R * owners(rng, T - 2 * N, CAPP - 2) + rng.integers(0, R, (N, T - 2 * N))], axis=1)
    if how == "full":
        lo = KR * int(rng.integers(N)) + int(rng.integers(T // 2, KR - N * R - T // 2 + 1)); K = lo + rng.permutation(N * R); rp = rng.permutation(N)
        G = np.stack([np.concatenate([R * h + rng.permutation(R)[:CAPP] for h in rp[:T // CAPP]]) for r in range(N)]); G[int(rng.integers(N)), :CAPP] = -1
    if how == "own":
        m = min(32, KR // R); c = int(rng.integers(m)); q = np.stack([rng.permutation(np.concatenate([2 * rng.permutation(KR // (2 * m))[:R // 2], 2 * rng.permutation(KR // (2 * m))[:R // 2] + 1])) for r in range(N)])
        pp = KR * ((np.arange(N) + int(rng.integers(1, N))) % N)[:, None] + m * q
        K = (pp + c).reshape(-1); O = (np.arange(N)[:, None] + 1 + np.arange(T) // 2 % (N - 1)) % N; O[:, :CAPP] = np.arange(N)[:, None]
        ev = np.stack([np.nonzero(v % 2 == 0)[0] for v in q]); G = R * O + ev[O, rng.integers(0, R // 2, (N, T))]; G[:, CAPP::2] = -1
    F = np.setdiff1d(np.arange(N * KR), K); Z = F[rng.integers(0, len(F), (N, T))]
    if how == "full": Z = np.tile(np.where(np.arange(T) % 2 == 0, lo - 1 - np.arange(T) // 2, lo + N * R + np.arange(T) // 2), (N, 1))
    if how == "own": Z = np.take_along_axis(pp, rng.integers(0, R, (N, T)), axis=1) + (c + rng.integers(1, m, (N, T))) % m
    if how == "absent":
        G[:, :T // 3] = -1; G[int(rng.integers(N))] = -1
        for j, d in ((0, 1), (1, -1)): nb = np.intersect1d(K + d, F); Z[:, j::4] = nb[rng.integers(0, len(nb), (N, T // 4))]
    W = np.where(G >= 0, K[np.maximum(G, 0)], Z); W = np.take_along_axis(W, np.argsort(rng.random((N, T)), axis=1), axis=1)
    return {"kb": np.stack([pack(k, 16) for k in K.reshape(N, R)]), "ka": np.stack([pack(w, 16) for w in W])}
def setup_inputs(rng):
    return dict({"tab": rng.standard_normal((N, 128, R), dtype=np.float32).astype(ml_dtypes.bfloat16)}, **lists(rng, "uniform"))
def setup_inputs_absent(rng):
    d = setup_inputs(rng); d.update(lists(rng, "absent"))
    for k in ("tab",): d[k] = (d[k].astype(np.float32) * 1048576.0).astype(d[k].dtype)
    return d
def setup_inputs_alike(rng):
    d = setup_inputs(rng); d.update(lists(rng, "alike"))
    for k in ("tab",): d[k] = (d[k].astype(np.float32) * (1 / 1024.0)).astype(d[k].dtype)
    return d
def setup_inputs_edge(rng):
    d = setup_inputs(rng); d.update(lists(rng, "edge"))
    return d
def setup_inputs_full(rng):
    d = setup_inputs(rng); d.update(lists(rng, "full"))
    return d
def setup_inputs_own(rng):
    d = setup_inputs(rng); d.update(lists(rng, "own"))
    return d
def check_inputs(x):
    bad = []
    if x["kb"].min() < 0 or x["kb"].max() >= N * KR: bad.append("kb out of range")
    if x["ka"].min() < 0 or x["ka"].max() >= N * KR: bad.append("ka out of range")
    if bad: return bad
    K = np.concatenate([entries(k) for k in x["kb"]]); H = np.full(N * KR, N); H[K] = np.arange(N * R) // R
    if len(np.unique(K)) < N * R: bad.append("a key stands twice in kb")
    if max(int(np.bincount(H[entries(a)], minlength=N + 1)[:N].max()) for a in x["ka"]) > CAPP: bad.append("more than CAPP entries of a list have their columns on one rank")
    return bad
def reference(tab, kb, ka):
    A = np.concatenate(list(tab) + [np.zeros((128, 1), tab.dtype)], axis=1)
    K, Q = np.concatenate([entries(k) for k in kb]), np.stack([entries(q) for q in ka])
    P = np.full(N * KR, N * R); P[K] = np.arange(N * R)
    return {"y": np.stack([A[:, P[Q[r]]] for r in range(N)])}

@@ -1,0 +1,433 @@
+from concourse.bass import DstId, RemoteDMATransfer
+from concourse.mybir import AluOpType, ActivationFunctionType
+
+N = 6
+R, T_ENT, CAPP = 4096, 1024, 256
+SIM = 80
+NCH = 4
+CW = R // NCH
+DUMP = 1024
+PADL, TABLE, PADR = 256, 24576, 16
+WALL = DUMP + PADL + TABLE + PADR
+ZS = 2048
+
+_COLS = {
+    "int32": {"KA": 64, "KAI": 192, "KBR": 256, "KB": 64, "KBI": 128, "PI": 4, "KI": 16, "KLH": 32},
+    "float32": {"KBE": 64, "KBT": 64, "CF": 4, "CM": 6, "P16": 8, "JN": 64, "J": 64, "C1": 64, "HQI": 4, "HQ": 4,
+                "RST": 16, "PS": 48, "PT": 48, "T1": 32, "VV": 16, "PEN": 16, "COL": 16, "KLF": 32, "FT": 16},
+    "bfloat16": {"X": 192, "W": WALL, "V": 1024, "G": N * T_ENT, "LI": 256, "SEL": 2, "I128": 128, "ML": 128,
+                 "BIAS": 256, "ONE": 192, "E": 768, "LT": 128, "MM": 16, "CUM": 16, "TAB": R, "DT": 2 * CAPP,
+                 "L": CAPP * (N + 1), "YT": T_ENT},
+    "float16": {"EH": 1024, "F": 16, "AH": 2048, "BH": 256, "SL": 8 * N, "SA": 40},
+    "uint16": {"OFB": 64, "OFQ": 384, "LST": 32, "SLU": 64},
+}
+SCRATCH = {"kaq": ("dram", [N, 128, 8], "int32")}
+for _d in _COLS:
+    for _n in _COLS[_d]:
+        SCRATCH[_n] = ("sbuf", [128, _COLS[_d][_n]], _d)
+for _n in ("PQ0", "PQ1", "PV", "PK", "PL", "PW"):
+    SCRATCH[_n] = ("psum", [128, 512], "float32")
+SEMAPHORES = ["ld_a", "ld_b", "ka_arr", "ka_rel", "ka_ld", "kb_arr", "go", "fz", "pt_arr", "sl_arr", "dt_arr", "st", "loc",
+              "cv", "cs", "cp", "ct"] + ["tl%d" % c for c in range(NCH)] + ["ta%d" % c for c in range(NCH)]
+_PLAN = {}
+
+
+def bits(m):
+    return [i for i in range(16) if (m >> i) & 1]
+
+
+def emask(engines):
+    return sum(1 << e for e in engines)
+
+
+def make_plan(cores, topo):
+    if _PLAN:
+        return _PLAN
+    teams = []
+    for s in cores:
+        team = [s] + [c for c in range(SIM) if c != s and topo.chip(c) == topo.chip(s) and topo.die(c) == topo.die(s)]
+        best = None
+        for own in [(s, a, b) for a in team[1:] for b in team[1:] if a != b]:
+            may = [[r for r in range(N) if cores[r] == o or topo.may_write(o, cores[r])] for o in own]
+            for q0 in [(x, y) for x in may[0] for y in may[0] if x < y]:
+                for q1 in [(x, y) for x in may[1] for y in may[1] if x < y and x not in q0 and y not in q0]:
+                    q2 = tuple(r for r in range(N) if r not in q0 + q1)
+                    if not all(r in may[2] for r in q2):
+                        continue
+                    sets = (q0, q1, q2)
+                    off = [sum(topo.chip(cores[r]) != topo.chip(s) for r in q) for q in sets]
+                    same = sum(topo.chip(cores[q[0]]) == topo.chip(cores[q[1]]) for q in sets)
+                    cost = (max(off), 0 if cores.index(s) in q0 else 1, off[0], same)
+                    if best is None or cost < best[0]:
+                        best = (cost, own, sets)
+
+        def far(r):
+            a, b = topo.chip(s), topo.chip(cores[r])
+            if a == b:
+                return 0 if cores[r] != s else -1
+            return 1 if (topo.mates(a, b) or topo.same_plane(a, b)) else 2
+        teams.append({"s": s, "team": team, "own": list(best[1]), "sets": [sorted(q, key=lambda r: -far(r)) for q in best[2]]})
+    everyone = [c for t in teams for c in t["team"]]
+    ka = {c: [] for c in everyone}
+    for r in range(N):
+        s, t = cores[r], teams[r]
+        near = [d for d in everyone if d != s and topo.chip(d) == topo.chip(s)]
+        direct = [d for d in everyone if d != s and d not in near and topo.may_write(s, d)]
+        rest = [d for d in everyone if d != s and d not in near and d not in direct]
+        call = []
+        eng = bits(topo.mask(s, near[0]))
+        if direct:
+            off = bits(topo.mask(s, direct[0]))
+            call.append((r, direct, off, "ka_arr"))
+            eng = [e for e in eng if e not in off]
+        else:
+            eng = eng[:len(eng) // 2]
+        if rest:
+            relay = [c for c in [t["own"][2], t["own"][1]] + t["team"] if c != s and all(topo.may_write(c, d) for d in rest)][0]
+            h = len(eng) // 2
+            call.insert(0, (r, [relay], eng[:h], "ka_rel"))
+            call.append((r, [d for d in near if d != relay], eng[h:], "ka_arr"))
+            ka[relay].append([(r, rest, bits(topo.mask(relay, rest[0])), "ka_arr")])
+        else:
+            call.append((r, near, eng, "ka_arr"))
+        ka[s].insert(0, call)
+    total = {}
+    for c in ka:
+        for call in ka[c]:
+            for (r, dsts, eng, sem) in call:
+                for d in dsts:
+                    total[(d, sem)] = total.get((d, sem), 0) + len(eng)
+    _PLAN.update({"teams": teams, "everyone": everyone, "ka": ka, "katotal": total})
+    return _PLAN
+
+
+def slot_engines(topo, src, dsts):
+    out, used = {}, []
+    for d in sorted(dsts, key=lambda c: len(bits(topo.mask(src, c)))):
+        out[d] = [e for e in bits(topo.mask(src, d)) if e not in used][:4]
+        used += out[d]
+    return out
+
+
+def rank_program(g, core, T, topo):
+    cores = list(T.cores)
+    P = make_plan(cores, topo)
+    if core not in P["everyone"]:
+        return
+    OP, COPY = AluOpType, ActivationFunctionType.Copy
+    si = [k for k in range(N) if core in P["teams"][k]["team"]][0]
+    t_ = P["teams"][si]
+    s, own, sets, team = t_["s"], t_["own"], t_["sets"], t_["team"]
+    mi = team.index(core)
+    is_rank = core == s
+    oi = own.index(core) if core in own else None
+    pos = [r for q in sets for r in q]
+
+    queue = {"v": g.vector, "s": g.scalar, "p": g, "t": g.tensor, "y": g.sync}
+    csem = {"v": "cv", "s": "cs", "p": "cp", "t": "ct"}
+    cnt = {"cv": 0, "cs": 0, "cp": 0, "ct": 0}
+    tot = {}
+    seen = {}
+
+    def need(q, *toks):
+        for sem, val in toks:
+            if seen.get((q, sem), 0) < val:
+                queue[q].wait_ge(T.sem[sem], val)
+                seen[(q, sem)] = val
+
+    def did(q, ins):
+        sem = csem[q]
+        ins.then_inc(T.sem[sem], 1)
+        cnt[sem] += 1
+        return (sem, cnt[sem])
+
+    def expect(sem, n):
+        tot[sem] = tot.get(sem, 0) + n
+        return (sem, tot[sem])
+
+    def dma(q, sem, out, in_):
+        queue[q].dma_start(out, in_).then_inc(T.sem[sem], 16)
+        return expect(sem, 16)
+
+    def send(transfers):
+        lst = []
+        for (d, e, sem, src, out) in transfers:
+            ids = []
+            for c in d:
+                rid, pid, _ = topo.addr(c)
+                ids.append(DstId(rid=rid, pnc=pid))
+            lst.append(RemoteDMATransfer(dst_ids=ids, dma_engine_mask=emask(e), remote_sem=T.sem[sem], srcs=[src],
+                                         dsts=[out for c in d]))
+            expect("loc", len(e))
+        g.remote_dma_fused(lst, local_sem=T.sem.loc)
+
+    def iota(out, pattern, base, cm):
+        return did("p", g.iota(out, pattern=pattern, base=base, channel_multiplier=cm, allow_small_or_imprecise_dtypes=True))
+
+    def ts(out, in0, s1, s2, op0, op1=None):
+        if op1 is None:
+            return did("v", g.vector.tensor_scalar(out, in0, s1, s2, op0))
+        return did("v", g.vector.tensor_scalar(out, in0, s1, s2, op0, op1))
+
+    def tt(out, in0, in1, op):
+        return did("v", g.vector.tensor_tensor(out, in0, in1, op))
+
+    def cp(out, in_):
+        return did("v", g.vector.tensor_copy(out, in_))
+
+    def fill(out, c):
+        return did("v", g.vector.memset(out, c))
+
+    def act(out, in_):
+        return did("s", g.scalar.activation(out, in_, COPY))
+
+    def mm(out, lhsT, rhs, start, stop):
+        return did("t", g.tensor.matmul(out, lhsT, rhs, start, stop))
+
+    if is_rank:
+        ld_a = dma("y", "ld_a", T.kaq[si], T.ka[:])
+        for k in range(8):
+            ld_b = dma("y" if k % 2 else "s", "ld_b", T.KBR[16 * k:16 * k + 16, :], T.kb[:])
+
+    c_pi = did("p", g.iota(T.PI[:, 3:4], pattern=[[0, 1]], base=0, channel_multiplier=1))
+    c_hq = iota(T.HQI[:], [[1, 4]], 4 * mi, 0)
+    c_jn = iota(T.JN[:], [[16, 64]], 0, 0)
+    c_li = iota(T.LI[:], [[1, 256]], 1, 0)
+
+    for n, call in enumerate(P["ka"][core]):
+        need("p", ld_a if is_rank and n == 0 else ("ka_rel", P["katotal"][(core, "ka_rel")]))
+        send([(d, e, sem, T.kaq[r], T.kaq[r]) for (r, d, e, sem) in call])
+    tk = [expect(sem, P["katotal"][(core, sem)]) for sem in ("ka_arr", "ka_rel") if (core, sem) in P["katotal"]]
+    if is_rank:
+        need("p", ld_b)
+        for i in range(1, len(team)):
+            send([([team[i]], bits(topo.mask(core, team[i])), "kb_arr", T.KBR[:, 64 * i:64 * i + 64], T.KB[:])])
+        g.sem_inc(T.sem.go, 1)
+        go = expect("go", 1)
+        kb_tok, KB = ld_b, T.KBR[:, 0:64]
+    else:
+        kb_tok, KB = expect("kb_arr", len(bits(topo.mask(s, core)))), T.KB[:]
+    c_p16 = iota(T.P16[:], [[-16, 8]], 0, 1)
+    c_i128 = iota(T.I128[:], [[0, 8], [1, 16]], 0, 0)
+    c_bias = iota(T.BIAS[:, 0:128], [[-32768, 8], [0, 16]], 0, 0)
+    if oi is not None:
+        c_ml = iota(T.ML[:], [[1, 128]], 0, 0)
+
+    z0 = fill(T.W[:, DUMP:DUMP + ZS], 0.0)
+    n_s, n_d = (4, 0) if is_rank else (3, 2)
+    at = DUMP + ZS
+    fills = []
+    for k in range(n_s):
+        need("s", z0)
+        fills.append(act(T.W[:, at:at + ZS], T.W[:, DUMP:DUMP + ZS]))
+        at += ZS
+    for k in range(n_d):
+        need("y", z0)
+        fz = dma("y", "fz", T.W[:, at:at + ZS], T.W[:, DUMP:DUMP + ZS])
+        at += ZS
+    if n_d:
+        fills.append(fz)
+
+    need("v", c_pi)
+    ts(T.PI[:, 0:1], T.PI[:, 3:4], 15, None, OP.bitwise_and)
+    ts(T.PI[:, 1:2], T.PI[:, 3:4], 4, None, OP.logical_shift_right)
+    a = ts(T.PI[:, 2:3], T.PI[:, 3:4], 31, None, OP.bitwise_and)
+    need("v", a)
+    cf = cp(T.CF[:], T.PI[:])
+    Q16, GRP, PIX = T.CF[:, 0:1], T.CF[:, 1:2], T.CF[:, 3:4]
+    need("v", cf)
+    ts(T.CM[:, 0:1], Q16, 8.0, None, OP.is_ge)
+    ts(T.CM[:, 1:2], Q16, 8.0, None, OP.is_lt)
+    ts(T.CM[:, 2:3], PIX, 0.0, None, OP.is_equal)
+    ts(T.CM[:, 3:4], Q16, 0.0, 256.0, OP.is_equal, OP.mult)
+    a = ts(T.CM[:, 4:5], Q16, 8.0, None, OP.is_equal)
+    need("v", a, c_jn)
+    ts(T.J[:], T.JN[:], Q16, None, OP.add)
+    need("v", c_hq)
+    c_h = ts(T.HQ[:], T.HQI[:], T.CM[:, 1:2], None, OP.mult)
+    c_sel = tt(T.SEL[:, 0:1], T.CM[:, 3:4], T.CM[:, 4:5], OP.add)
+    need("v", c_h, c_li)
+    ts(T.C1[:], T.J[:], -1.0, float(DUMP + PADL), OP.mult, OP.add)
+    for k in range(4):
+        ts(T.V[:, 256 * k:256 * k + 256], T.LI[:], T.CM[:, 0:1], T.HQ[:, k:k + 1], OP.mult, OP.add)
+    fill(T.ONE[:], 1.0)
+    fill(T.W[:, at:WALL], 0.0)
+
+    need("v", kb_tok)
+    ts(T.KBI[:, 0:64], KB, 7, None, OP.bitwise_and)
+    a = ts(T.KBI[:, 64:128], KB, 3, None, OP.logical_shift_right)
+    need("v", a)
+    ts(T.KBE[:], T.KBI[:, 0:64], GRP, None, OP.is_equal)
+    a = tt(T.KBT[:], T.KBI[:, 64:128], T.C1[:], OP.add)
+    need("v", a)
+    a = tt(T.KBT[:], T.KBE[:], T.KBT[:], OP.mult)
+    need("v", a)
+    a = tt(T.KBT[:], T.KBT[:], T.J[:], OP.add)
+    need("v", a)
+    a = cp(T.OFB[:], T.KBT[:])
+    need("v", a, *fills)
+    scat = cp(T.W[:, 0:WALL].indirect(T.OFB[:]), T.V[:])
+    need("v", c_i128, c_bias, c_p16)
+    c_bi = ts(T.BIAS[:, 128:256], T.BIAS[:, 0:128], T.CM[:, 2:3], None, OP.mult)
+    for r in range(N):
+        c_e = ts(T.E[:, 128 * r:128 * r + 128], T.I128[:], T.P16[:, r:r + 1], None, OP.is_equal)
+
+    if is_rank:
+        need("y", go)
+        for c in range(NCH // 2):
+            dma("y", "tl%d" % c, T.TAB[:, c * CW:c * CW + CW], T.tab[:, c * CW:c * CW + CW])
+        need("y", ld_a)
+    need("y", *tk)
+    ka_ld = dma("y", "ka_ld", T.KA[0:96, :], T.kaq[:])
+    if is_rank:
+        for c in range(NCH // 2, NCH):
+            dma("y", "tl%d" % c, T.TAB[:, c * CW:c * CW + CW], T.tab[:, c * CW:c * CW + CW])
+    need("t", c_bi)
+    PQ = [T.PQ0, T.PQ1]
+    for h in (1, 0):
+        mm(PQ[h][:, 0:192], T.BIAS[0:96, 128:256], T.ONE[0:96, :], True, False)
+    need("v", ka_ld)
+    ts(T.KAI[0:96, 0:64], T.KA[0:96, :], 7, None, OP.bitwise_and)
+    ts(T.KAI[0:96, 64:128], T.KA[0:96, :], 11, None, OP.logical_shift_right)
+    a = ts(T.KAI[0:96, 128:192], T.KA[0:96, :], 3, 255, OP.logical_shift_right, OP.bitwise_and)
+    need("v", a)
+    ts(T.X[0:96, 0:64], T.KAI[0:96, 0:64], 32768.0, None, OP.mult)
+    ts(T.X[0:96, 64:128], T.KAI[0:96, 64:128], 256.0, float(PADL), OP.mult, OP.add)
+    a = cp(T.X[0:96, 128:192], T.KAI[0:96, 128:192])
+    need("t", a, c_e)
+    off_tok = [None, None]
+    for h in (1, 0):
+        for k in range(3):
+            r = pos[3 * h + k]
+            for x in range(3):
+                m = mm(PQ[h][:, 64 * k:64 * k + 64], T.E[0:96, 128 * r:128 * r + 128], T.X[0:96, 64 * x:64 * x + 64],
+                       False, k == 2 and x == 2)
+        need("v", m)
+        off_tok[h] = ts(T.OFQ[:, 192 * h:192 * h + 192], PQ[h][:, 0:192], 0.0, float(PADL + TABLE), OP.max, OP.min)
+
+    got = []
+    need("s", off_tok[1], scat)
+    need("v", off_tok[0], scat)
+    for (x, y) in ((0, 1024), (1024, 2048), (2048, 2560), (2560, 3072)):
+        o = 192 + x // 16
+        got.append((act(T.G[:, 3072 + x:3072 + y], T.W[:, DUMP:WALL].indirect(T.OFQ[:, o:o + (y - x) // 16])), 3072 + x, 3072 + y))
+        got.append((cp(T.G[:, x:y], T.W[:, DUMP:WALL].indirect(T.OFQ[:, x // 16:y // 16])), x, y))
+    need("t", c_sel)
+    for (tok, x, y) in got:
+        need("t", tok)
+        for c in range(x // 128, y // 128):
+            m = mm(T.PV[:, c:c + 1], T.G[:, 128 * c:128 * c + 128], T.SEL[:, 0:1], True, True)
+    need("v", m)
+    ps = cp(T.PS[:], T.PV[:, 0:48])
+
+    tab_tok = []
+    if oi is not None:
+        for c in range(NCH):
+            tok = ("tl%d" % c, 16) if is_rank else expect("ta%d" % c, len(bits(topo.mask(own[oi - 1], core))))
+            tab_tok.append(tok)
+            if oi < 2:
+                need("p", tok)
+                blk = T.TAB[:, c * CW:c * CW + CW]
+                send([([own[oi + 1]], bits(topo.mask(core, own[oi + 1])), "ta%d" % c, blk, blk)])
+
+    need("p", ps)
+    to = [c for c in own if c != core]
+    tr = []
+    for j, d in enumerate(to):
+        n = 8 if len(to) == 2 else 4
+        k, slot = own.index(d), [c for c in team if c != d].index(core)
+        tr.append(([d], bits(topo.mask(core, d))[n * j:n * j + n], "pt_arr", T.PS[:, 16 * k:16 * k + 16],
+                   T.PT[:, 16 * slot:16 * slot + 16]))
+    send(tr)
+
+    if oi is not None:
+        reqs = sets[oi]
+        need("v", c_ml)
+        c_lt = ts(T.LT[:], T.ML[:], PIX, -1.0, OP.is_le, OP.mult)
+        a = fill(T.RST[:], 1.0)
+        need("v", a)
+        for rr in range(2):
+            fill(T.RST[:, 8 * rr:8 * rr + 1], 0.0)
+        if is_rank:
+            fill(T.L[:, 0:CAPP], 0.0)
+            for b in range(8):
+                ts(T.EH[:, 128 * b:128 * b + 128], T.I128[:], T.P16[:, b:b + 1], None, OP.is_equal)
+        need("v", ("cv", cnt["cv"]), expect("pt_arr", sum(8 if c in own else 4 for c in team if c != core)))
+        tt(T.T1[:, 0:16], T.PT[:, 0:16], T.PT[:, 16:32], OP.add)
+        a = tt(T.T1[:, 16:32], T.PT[:, 32:48], T.PS[:, 16 * oi:16 * oi + 16], OP.add)
+        need("v", a)
+        a = tt(T.VV[:], T.T1[:, 0:16], T.T1[:, 16:32], OP.add)
+        need("v", a)
+        hit = ts(T.MM[:], T.VV[:], 0.5, None, OP.is_ge)
+        need("v", hit)
+        cum = did("v", g.vector.tensor_tensor_scan(T.CUM[:], T.RST[:], T.MM[:], 0.0, OP.mult, OP.add))
+        ts(T.PEN[:], T.VV[:], 0.5, 4096.0, OP.is_lt, OP.mult)
+        col = ts(T.COL[:], T.VV[:], -2049.0, None, OP.add)
+        need("t", c_lt, hit)
+        mm(T.PK[:, 0:16], T.LT[:], T.MM[:], True, False)
+        need("t", cum)
+        pk = mm(T.PK[:, 0:16], T.ONE[:, 0:128], T.CUM[:], False, True)
+        need("v", pk, col)
+        a = tt(T.KI[:], T.PK[:, 0:16], T.PEN[:], OP.add)
+        ft = ts(T.FT[:], T.PK[:, 0:16], float(CAPP * (si + 1)), None, OP.add)
+        need("v", a)
+        ts(T.KLH[:, 0:16], T.KI[:], 15, None, OP.bitwise_and)
+        a = ts(T.KLH[:, 16:32], T.KI[:], 4, None, OP.logical_shift_right)
+        need("v", ft)
+        for rr, r in enumerate(reqs):
+            out = T.SL[:, 8 * si:8 * si + 8] if cores[r] == core else T.F[:, 8 * rr:8 * rr + 8]
+            ff = tt(out, T.FT[:, 8 * rr:8 * rr + 8], T.MM[:, 8 * rr:8 * rr + 8], OP.mult)
+        need("v", a)
+        a = cp(T.KLF[:], T.KLH[:])
+        need("p", ff)
+        se = slot_engines(topo, core, [cores[r] for r in reqs if cores[r] != core])
+        send([([cores[r]], se[cores[r]], "sl_arr", T.F[:, 8 * rr:8 * rr + 8], T.SL[:, 8 * si:8 * si + 8])
+              for rr, r in enumerate(reqs) if cores[r] != core])
+        need("v", a)
+        for c in range(16):
+            rr = c // 8
+            ts(T.AH[:, 128 * c:128 * c + 128], T.I128[:], T.KLF[:, c:c + 1], None, OP.is_equal)
+            b = ts(T.BH[:, 16 * c:16 * c + 16], T.I128[:, 0:16], T.KLF[:, 16 + c:17 + c], T.COL[:, c:c + 1], OP.is_equal, OP.mult)
+            need("t", b)
+            m = mm(T.PL[:, 16 * rr:16 * rr + 16], T.AH[:, 128 * c:128 * c + 128], T.BH[:, 16 * c:16 * c + 16], c % 8 == 0, c % 8 == 7)
+        need("v", m)
+        a = ts(T.LST[:], T.PL[:, 0:32], 2048.0, None, OP.add)
+        need("v", a, *tab_tok)
+        for rr, r in enumerate(reqs):
+            here = cores[r] == core
+            land = T.L[:, CAPP * (si + 1):CAPP * (si + 2)]
+            out = land if here else T.DT[:, CAPP * rr:CAPP * rr + CAPP]
+            d = cp(out, T.TAB[:].indirect(T.LST[:, 16 * rr:16 * rr + 16]))
+            if not here:
+                need("p", d)
+                send([([cores[r]], bits(topo.mask(core, cores[r])), "dt_arr", out, land)])
+
+    if is_rank:
+        sl_n = dt_n = 0
+        for tm in P["teams"]:
+            for src, q in zip(tm["own"], tm["sets"]):
+                if si in q and src != core:
+                    sl_n += len(slot_engines(topo, src, [cores[r] for r in q if cores[r] != src])[core])
+                    dt_n += len(bits(topo.mask(src, core)))
+        need("v", expect("sl_arr", sl_n), ("cv", cnt["cv"]))
+        a = tt(T.SA[:, 0:24], T.SL[:, 0:24], T.SL[:, 24:48], OP.add)
+        need("v", a)
+        a = tt(T.SA[:, 24:32], T.SA[:, 0:8], T.SA[:, 8:16], OP.add)
+        need("v", a)
+        a = tt(T.SA[:, 32:40], T.SA[:, 24:32], T.SA[:, 16:24], OP.add)
+        need("t", a)
+        for b in range(8):
+            m = mm(T.PW[:, b:64:8], T.EH[:, 128 * b:128 * b + 128], T.SA[:, 32:40], True, True)
+        need("v", m)
+        a = cp(T.SLU[:], T.PW[:, 0:64])
+        need("v", a, expect("dt_arr", dt_n))
+        for h in range(2):
+            yt = cp(T.YT[:, 512 * h:512 * h + 512], T.L[:].indirect(T.SLU[:, 32 * h:32 * h + 32]))
+            need("ys"[h], yt)
+            dma("ys"[h], "st", T.y[:, 512 * h:512 * h + 512], T.YT[:, 512 * h:512 * h + 512])
+
+    for sem in tot:
+        need("p", (sem, tot[sem]))
+    for sem in cnt:
+        if cnt[sem]:
+            need("p", (sem, cnt[sem]))

@@ -5,27 +5,30 @@ N = 6
 R, T_ENT, CAPP = 4096, 1024, 256
 SIM = 80
 NCH = 4
+N_EARLY = 2
+BEFORE = (4, 2)
 CW = R // NCH
-DUMP = 1024
-PADL, TABLE, PADR = 256, 24576, 16
+NC_RANK, NC_HELP = 46, 70
+DUMP = 16 * NC_HELP
+PADL, TABLE, PADR = 8, 24576, 16
 WALL = DUMP + PADL + TABLE + PADR
 ZS = 2048
 
 _COLS = {
-    "int32": {"KA": 64, "KAI": 192, "KBR": 256, "KB": 64, "KBI": 128, "PI": 4, "KI": 16, "KLH": 32},
-    "float32": {"KBE": 64, "KBT": 64, "CF": 4, "CM": 6, "P16": 8, "JN": 64, "J": 64, "C1": 64, "HQI": 4, "HQ": 4,
+    "int32": {"KA": 64, "KAI": 192, "KBR": 256, "KB": NC_HELP, "KBI": 2 * NC_HELP, "PI": 4, "KI": 16, "KLH": 32},
+    "float32": {"KBE": NC_HELP, "KBT": NC_HELP, "CF": 4, "CM": 6, "P16": 8, "JN": NC_HELP, "J": NC_HELP, "C1": NC_HELP, "HQ": 8,
                 "RST": 16, "PS": 48, "PT": 48, "T1": 32, "VV": 16, "PEN": 16, "COL": 16, "KLF": 32, "FT": 16},
-    "bfloat16": {"X": 192, "W": WALL, "V": 1024, "G": N * T_ENT, "LI": 256, "SEL": 2, "I128": 128, "ML": 128,
-                 "BIAS": 256, "ONE": 192, "E": 768, "LT": 128, "MM": 16, "CUM": 16, "TAB": R, "DT": 2 * CAPP,
+    "bfloat16": {"X": 192, "W": WALL, "V": 16 * NC_HELP, "G": N * T_ENT, "LI": 256, "SEL": 2, "I128": 128, "ML": 128,
+                 "BIAS": 256, "ONE": 128, "E": 768, "LT": 128, "MM": 16, "CUM": 16, "TAB": R, "DT": 2 * CAPP,
                  "L": CAPP * (N + 1), "YT": T_ENT},
     "float16": {"EH": 1024, "F": 16, "AH": 2048, "BH": 256, "SL": 8 * N, "SA": 40},
-    "uint16": {"OFB": 64, "OFQ": 384, "LST": 32, "SLU": 64},
+    "uint16": {"OFB": NC_HELP, "OFQ": 384, "LST": 32, "SLU": 64},
 }
 SCRATCH = {"kaq": ("dram", [N, 128, 8], "int32")}
 for _d in _COLS:
     for _n in _COLS[_d]:
         SCRATCH[_n] = ("sbuf", [128, _COLS[_d][_n]], _d)
-for _n in ("PQ0", "PQ1", "PV", "PK", "PL", "PW"):
+for _n in ("PQ0", "PQ1", "PX", "PV", "PK", "PL", "PW"):
     SCRATCH[_n] = ("psum", [128, 512], "float32")
 SEMAPHORES = ["ld_a", "ld_b", "ka_arr", "ka_rel", "ka_ld", "kb_arr", "go", "fz", "pt_arr", "sl_arr", "dt_arr", "st", "loc",
               "cv", "cs", "cp", "ct"] + ["tl%d" % c for c in range(NCH)] + ["ta%d" % c for c in range(NCH)]
@@ -71,26 +74,28 @@ def make_plan(cores, topo):
     ka = {c: [] for c in everyone}
     for r in range(N):
         s, t = cores[r], teams[r]
-        near = [d for d in everyone if d != s and topo.chip(d) == topo.chip(s)]
-        direct = [d for d in everyone if d != s and d not in near and topo.may_write(s, d)]
-        rest = [d for d in everyone if d != s and d not in near and d not in direct]
-        call = []
-        eng = bits(topo.mask(s, near[0]))
+        mates = t["team"][1:]
+        near = [d for d in everyone if d not in t["team"] and topo.chip(d) == topo.chip(s)]
+        away = [d for d in everyone if topo.chip(d) != topo.chip(s)]
+        direct = [d for d in away if topo.may_write(s, d)]
+        rest = [d for d in away if d not in direct]
+        off = bits(topo.mask(s, away[0]))
+        eng = [e for e in bits(topo.mask(s, mates[0])) if e not in off][:4]
+        call = [(r, mates, eng, "ka_rel")]
         if direct:
-            off = bits(topo.mask(s, direct[0]))
             call.append((r, direct, off, "ka_arr"))
-            eng = [e for e in eng if e not in off]
-        else:
-            eng = eng[:len(eng) // 2]
-        if rest:
-            relay = [c for c in [t["own"][2], t["own"][1]] + t["team"] if c != s and all(topo.may_write(c, d) for d in rest)][0]
-            h = len(eng) // 2
-            call.insert(0, (r, [relay], eng[:h], "ka_rel"))
-            call.append((r, [d for d in near if d != relay], eng[h:], "ka_arr"))
-            ka[relay].append([(r, rest, bits(topo.mask(relay, rest[0])), "ka_arr")])
-        else:
-            call.append((r, near, eng, "ka_arr"))
         ka[s].insert(0, call)
+        third = [c for c in t["team"] if c not in t["own"]]
+        if rest:
+            ports = [c for c in t["own"][1:] if all(topo.may_write(c, d) for d in rest)]
+            for k, c in enumerate(ports):
+                ka[c].append([(r, rest[k::len(ports)], bits(topo.mask(c, rest[0])), "ka_arr")])
+        third.append(t["own"][2])
+        for k, c in enumerate(third):
+            eng = bits(topo.mask(c, near[0]))
+            if ka[c]:
+                eng = [e for e in eng if e not in off]
+            ka[c].append([(r, near[k::len(third)], eng, "ka_arr")])
     total = {}
     for c in ka:
         for call in ka[c]:
@@ -101,12 +106,16 @@ def make_plan(cores, topo):
     return _PLAN
 
 
-def slot_engines(topo, src, dsts):
-    out, used = {}, []
-    for d in sorted(dsts, key=lambda c: len(bits(topo.mask(src, c)))):
-        out[d] = [e for e in bits(topo.mask(src, d)) if e not in used][:4]
-        used += out[d]
-    return out
+def split_engines(topo, src, dsts, most):
+    dsts = sorted(dsts, key=lambda c: len(bits(topo.mask(src, c))))
+    a = bits(topo.mask(src, dsts[0]))
+    if len(dsts) == 1:
+        return {dsts[0]: a[:most]}
+    b = [e for e in bits(topo.mask(src, dsts[1])) if e not in a]
+    if not b:
+        h = len(a) // 2
+        a, b = a[:h], a[h:]
+    return {dsts[0]: a[:most], dsts[1]: b[:most]}
 
 
 def rank_program(g, core, T, topo):
@@ -120,6 +129,8 @@ def rank_program(g, core, T, topo):
     s, own, sets, team = t_["s"], t_["own"], t_["sets"], t_["team"]
     mi = team.index(core)
     is_rank = core == s
+    nc = NC_RANK if is_rank else NC_HELP
+    c0 = 0 if is_rank else NC_RANK + NC_HELP * (mi - 1)
     oi = own.index(core) if core in own else None
     pos = [r for q in sets for r in q]
 
@@ -164,6 +175,9 @@ def rank_program(g, core, T, topo):
     def iota(out, pattern, base, cm):
         return did("p", g.iota(out, pattern=pattern, base=base, channel_multiplier=cm, allow_small_or_imprecise_dtypes=True))
 
+    def select(out, in_, pattern, op, fill_, base, cm):
+        return did("p", g.affine_select(out, in_, pattern=pattern, compare_op=op, fill=fill_, base=base, channel_multiplier=cm))
+
     def ts(out, in0, s1, s2, op0, op1=None):
         if op1 is None:
             return did("v", g.vector.tensor_scalar(out, in0, s1, s2, op0))
@@ -179,7 +193,7 @@ def rank_program(g, core, T, topo):
         return did("v", g.vector.memset(out, c))
 
     def act(out, in_):
-        return did("s", g.scalar.activation(out, in_, COPY))
+        return did("s", g.scalar.activation(out, in_, COPY, bias=-0.0))
 
     def mm(out, lhsT, rhs, start, stop):
         return did("t", g.tensor.matmul(out, lhsT, rhs, start, stop))
@@ -188,41 +202,49 @@ def rank_program(g, core, T, topo):
         ld_a = dma("y", "ld_a", T.kaq[si], T.ka[:])
         for k in range(8):
             ld_b = dma("y" if k % 2 else "s", "ld_b", T.KBR[16 * k:16 * k + 16, :], T.kb[:])
+    z0 = fill(T.W[:, DUMP:DUMP + ZS // 2], 0.0)
+    z1 = fill(T.W[:, DUMP + ZS // 2:DUMP + ZS], 0.0)
 
     c_pi = did("p", g.iota(T.PI[:, 3:4], pattern=[[0, 1]], base=0, channel_multiplier=1))
-    c_hq = iota(T.HQI[:], [[1, 4]], 4 * mi, 0)
-    c_jn = iota(T.JN[:], [[16, 64]], 0, 0)
+    c_hq = iota(T.HQ[:], [[16, 8]], c0, 0)
+    c_jn = iota(T.JN[:], [[16, NC_HELP]], 0, 0)
     c_li = iota(T.LI[:], [[1, 256]], 1, 0)
-
     for n, call in enumerate(P["ka"][core]):
         need("p", ld_a if is_rank and n == 0 else ("ka_rel", P["katotal"][(core, "ka_rel")]))
         send([(d, e, sem, T.kaq[r], T.kaq[r]) for (r, d, e, sem) in call])
     tk = [expect(sem, P["katotal"][(core, sem)]) for sem in ("ka_arr", "ka_rel") if (core, sem) in P["katotal"]]
+    on = bits(topo.mask(s, team[1]))
+    kb_eng = [None, on[:8], on[8:12], on[12:]]
     if is_rank:
         need("p", ld_b)
-        for i in range(1, len(team)):
-            send([([team[i]], bits(topo.mask(core, team[i])), "kb_arr", T.KBR[:, 64 * i:64 * i + 64], T.KB[:])])
+        send([([team[i]], kb_eng[i], "kb_arr", T.KBR[:, NC_RANK + NC_HELP * (i - 1):NC_RANK + NC_HELP * i], T.KB[:])
+              for i in range(1, 4)])
         g.sem_inc(T.sem.go, 1)
         go = expect("go", 1)
-        kb_tok, KB = ld_b, T.KBR[:, 0:64]
+        kb_tok, KB = ld_b, T.KBR[:, 0:nc]
     else:
-        kb_tok, KB = expect("kb_arr", len(bits(topo.mask(s, core)))), T.KB[:]
-    c_p16 = iota(T.P16[:], [[-16, 8]], 0, 1)
-    c_i128 = iota(T.I128[:], [[0, 8], [1, 16]], 0, 0)
+        kb_tok, KB = expect("kb_arr", len(kb_eng[mi])), T.KB[:]
     c_bias = iota(T.BIAS[:, 0:128], [[-32768, 8], [0, 16]], 0, 0)
+    need("p", z0)
+    c_e = select(T.E[0:96, :], T.W[0:96, DUMP:DUMP + 768], [[-16, 6], [0, 8], [-1, 16]], OP.not_equal, 1.0, 0, 1)
+    need("p", c_bias)
+    c_bi = select(T.BIAS[:, 128:256], T.BIAS[:, 0:128], [[0, 128]], OP.is_equal, 0.0, 0, 1)
+    need("p", c_bi)
+    c_bi = select(T.BIAS[:, 128:256], T.BIAS[:, 128:256], [[0, 128]], OP.not_equal, float(PADL), -1, 1)
     if oi is not None:
+        c_i128 = iota(T.I128[:], [[0, 8], [1, 16]], 0, 0)
+        c_p16 = iota(T.P16[:], [[-16, 8]], 0, 1)
         c_ml = iota(T.ML[:], [[1, 128]], 0, 0)
 
-    z0 = fill(T.W[:, DUMP:DUMP + ZS], 0.0)
-    n_s, n_d = (4, 0) if is_rank else (3, 2)
+    w_s, n_d = ([1024] * 8 + [512], 0) if is_rank else ([1024] * 7, 2)
     at = DUMP + ZS
-    fills = []
-    for k in range(n_s):
-        need("s", z0)
-        fills.append(act(T.W[:, at:at + ZS], T.W[:, DUMP:DUMP + ZS]))
-        at += ZS
+    fills = [c_e]
+    need("s", z0)
+    for w in w_s:
+        fills.append(act(T.W[:, at:at + w], T.W[:, DUMP:DUMP + w]))
+        at += w
     for k in range(n_d):
-        need("y", z0)
+        need("y", z1)
         fz = dma("y", "fz", T.W[:, at:at + ZS], T.W[:, DUMP:DUMP + ZS])
         at += ZS
     if n_d:
@@ -231,89 +253,105 @@ def rank_program(g, core, T, topo):
     need("v", c_pi)
     ts(T.PI[:, 0:1], T.PI[:, 3:4], 15, None, OP.bitwise_and)
     ts(T.PI[:, 1:2], T.PI[:, 3:4], 4, None, OP.logical_shift_right)
-    a = ts(T.PI[:, 2:3], T.PI[:, 3:4], 31, None, OP.bitwise_and)
+    a = ts(T.PI[:, 2:3], T.PI[:, 3:4], 8, None, OP.bitwise_and)
     need("v", a)
     cf = cp(T.CF[:], T.PI[:])
-    Q16, GRP, PIX = T.CF[:, 0:1], T.CF[:, 1:2], T.CF[:, 3:4]
+    Q16, GRP, Q8, PIX = T.CF[:, 0:1], T.CF[:, 1:2], T.CF[:, 2:3], T.CF[:, 3:4]
     need("v", cf)
-    ts(T.CM[:, 0:1], Q16, 8.0, None, OP.is_ge)
-    ts(T.CM[:, 1:2], Q16, 8.0, None, OP.is_lt)
-    ts(T.CM[:, 2:3], PIX, 0.0, None, OP.is_equal)
-    ts(T.CM[:, 3:4], Q16, 0.0, 256.0, OP.is_equal, OP.mult)
-    a = ts(T.CM[:, 4:5], Q16, 8.0, None, OP.is_equal)
-    need("v", a, c_jn)
+    ts(T.CM[:, 0:1], Q8, 0.125, None, OP.mult)
+    a = ts(T.CM[:, 1:2], Q8, -0.125, 1.0, OP.mult, OP.add)
+    need("v", a, c_jn, c_hq)
     ts(T.J[:], T.JN[:], Q16, None, OP.add)
-    need("v", c_hq)
-    c_h = ts(T.HQ[:], T.HQI[:], T.CM[:, 1:2], None, OP.mult)
-    c_sel = tt(T.SEL[:, 0:1], T.CM[:, 3:4], T.CM[:, 4:5], OP.add)
-    need("v", c_h, c_li)
+    a = ts(T.HQ[:], T.HQ[:], T.CM[:, 1:2], None, OP.mult)
+    need("v", a, c_li)
     ts(T.C1[:], T.J[:], -1.0, float(DUMP + PADL), OP.mult, OP.add)
-    for k in range(4):
-        ts(T.V[:, 256 * k:256 * k + 256], T.LI[:], T.CM[:, 0:1], T.HQ[:, k:k + 1], OP.mult, OP.add)
-    fill(T.ONE[:], 1.0)
+    for k in range((nc + 15) // 16):
+        w = min(256, 16 * nc - 256 * k)
+        ts(T.V[:, 256 * k:256 * k + w], T.LI[:, 0:w], T.CM[:, 0:1], T.HQ[:, k:k + 1], OP.mult, OP.add)
+    c_one = fill(T.ONE[:], 1.0)
     fill(T.W[:, at:WALL], 0.0)
 
     need("v", kb_tok)
-    ts(T.KBI[:, 0:64], KB, 7, None, OP.bitwise_and)
-    a = ts(T.KBI[:, 64:128], KB, 3, None, OP.logical_shift_right)
+    k7, k3, e, t, j = T.KBI[:, 0:nc], T.KBI[:, NC_HELP:NC_HELP + nc], T.KBE[:, 0:nc], T.KBT[:, 0:nc], T.J[:, 0:nc]
+    ts(k7, KB, 7, None, OP.bitwise_and)
+    a = ts(k3, KB, 3, None, OP.logical_shift_right)
     need("v", a)
-    ts(T.KBE[:], T.KBI[:, 0:64], GRP, None, OP.is_equal)
-    a = tt(T.KBT[:], T.KBI[:, 64:128], T.C1[:], OP.add)
+    ts(e, k7, GRP, None, OP.is_equal)
+    a = tt(t, k3, T.C1[:, 0:nc], OP.add)
     need("v", a)
-    a = tt(T.KBT[:], T.KBE[:], T.KBT[:], OP.mult)
+    a = tt(t, e, t, OP.mult)
     need("v", a)
-    a = tt(T.KBT[:], T.KBT[:], T.J[:], OP.add)
+    a = tt(t, t, j, OP.add)
     need("v", a)
-    a = cp(T.OFB[:], T.KBT[:])
+    a = cp(T.OFB[:, 0:nc], t)
     need("v", a, *fills)
-    scat = cp(T.W[:, 0:WALL].indirect(T.OFB[:]), T.V[:])
-    need("v", c_i128, c_bias, c_p16)
-    c_bi = ts(T.BIAS[:, 128:256], T.BIAS[:, 0:128], T.CM[:, 2:3], None, OP.mult)
-    for r in range(N):
-        c_e = ts(T.E[:, 128 * r:128 * r + 128], T.I128[:], T.P16[:, r:r + 1], None, OP.is_equal)
+    scat = cp(T.W[:, 0:WALL].indirect(T.OFB[:, 0:nc]), T.V[:, 0:16 * nc])
+
+    def tab_load(lo, hi):
+        for c in range(lo, hi):
+            dma("y", "tl%d" % c, T.TAB[:, c * CW:c * CW + CW], T.tab[:, c * CW:c * CW + CW])
 
     if is_rank:
         need("y", go)
-        for c in range(NCH // 2):
-            dma("y", "tl%d" % c, T.TAB[:, c * CW:c * CW + CW], T.tab[:, c * CW:c * CW + CW])
+        tab_load(0, N_EARLY)
         need("y", ld_a)
     need("y", *tk)
     ka_ld = dma("y", "ka_ld", T.KA[0:96, :], T.kaq[:])
     if is_rank:
-        for c in range(NCH // 2, NCH):
-            dma("y", "tl%d" % c, T.TAB[:, c * CW:c * CW + CW], T.tab[:, c * CW:c * CW + CW])
-    need("t", c_bi)
-    PQ = [T.PQ0, T.PQ1]
-    for h in (1, 0):
-        mm(PQ[h][:, 0:192], T.BIAS[0:96, 128:256], T.ONE[0:96, :], True, False)
+        tab_load(N_EARLY, NCH)
+    need("t", c_one, c_bi)
+    PQ = [T.PQ0, T.PQ1, T.PX, T.PK, T.PL, T.PW]
+    ORDER = (3, 0, 4, 5, 1, 2)
+    for k in ORDER:
+        mm(PQ[k][:, 0:64], T.BIAS[0:96, 128:256], T.ONE[0:96, 0:64], True, False)
     need("v", ka_ld)
     ts(T.KAI[0:96, 0:64], T.KA[0:96, :], 7, None, OP.bitwise_and)
     ts(T.KAI[0:96, 64:128], T.KA[0:96, :], 11, None, OP.logical_shift_right)
     a = ts(T.KAI[0:96, 128:192], T.KA[0:96, :], 3, 255, OP.logical_shift_right, OP.bitwise_and)
     need("v", a)
     ts(T.X[0:96, 0:64], T.KAI[0:96, 0:64], 32768.0, None, OP.mult)
-    ts(T.X[0:96, 64:128], T.KAI[0:96, 64:128], 256.0, float(PADL), OP.mult, OP.add)
+    ts(T.X[0:96, 64:128], T.KAI[0:96, 64:128], 256.0, None, OP.mult)
     a = cp(T.X[0:96, 128:192], T.KAI[0:96, 128:192])
     need("t", a, c_e)
-    off_tok = [None, None]
-    for h in (1, 0):
-        for k in range(3):
-            r = pos[3 * h + k]
-            for x in range(3):
-                m = mm(PQ[h][:, 64 * k:64 * k + 64], T.E[0:96, 128 * r:128 * r + 128], T.X[0:96, 64 * x:64 * x + 64],
-                       False, k == 2 and x == 2)
-        need("v", m)
-        off_tok[h] = ts(T.OFQ[:, 192 * h:192 * h + 192], PQ[h][:, 0:192], 0.0, float(PADL + TABLE), OP.max, OP.min)
+    spread = {}
+    for k in ORDER:
+        r = pos[k]
+        for x in range(3):
+            spread[k] = mm(PQ[k][:, 0:64], T.E[0:96, 128 * r:128 * r + 128], T.X[0:96, 64 * x:64 * x + 64], False, x == 2)
+    ts(T.CM[:, 3:4], Q16, 0.0, 16.0, OP.is_equal, OP.mult)
+    a = ts(T.CM[:, 4:5], Q16, 8.0, None, OP.is_equal)
+    need("v", a)
+    c_sel = tt(T.SEL[:, 0:1], T.CM[:, 3:4], T.CM[:, 4:5], OP.add)
 
-    got = []
-    need("s", off_tok[1], scat)
-    need("v", off_tok[0], scat)
-    for (x, y) in ((0, 1024), (1024, 2048), (2048, 2560), (2560, 3072)):
-        o = 192 + x // 16
-        got.append((act(T.G[:, 3072 + x:3072 + y], T.W[:, DUMP:WALL].indirect(T.OFQ[:, o:o + (y - x) // 16])), 3072 + x, 3072 + y))
-        got.append((cp(T.G[:, x:y], T.W[:, DUMP:WALL].indirect(T.OFQ[:, x // 16:y // 16])), x, y))
+    def offsets(k):
+        need("v", spread[k])
+        return ts(T.OFQ[:, 64 * k:64 * k + 64], PQ[k][:, 0:64], 0.0, float(PADL + TABLE), OP.max, OP.min)
+
+    TBL = T.W[:, DUMP:WALL]
+    off_tok, got = {}, {}
+
+    def look(q, k, parts):
+        got[k] = []
+        n = T_ENT // parts
+        need(q, off_tok[k], scat)
+        for x in range(T_ENT * k, T_ENT * k + T_ENT, n):
+            o = T.OFQ[:, x // 16:(x + n) // 16]
+            tok = act(T.G[:, x:x + n], TBL.indirect(o)) if q == "s" else cp(T.G[:, x:x + n], TBL.indirect(o))
+            got[k].append((tok, x, x + n))
+
+    for k in (3, 0, 4):
+        off_tok[k] = offsets(k)
+    look("v", 0, 1)
+    for k in (5, 1):
+        off_tok[k] = offsets(k)
+    look("v", 1, 1)
+    off_tok[2] = offsets(2)
+    look("v", 2, 2)
+    look("s", 3, 1)
+    look("s", 4, 1)
+    look("s", 5, 2)
     need("t", c_sel)
-    for (tok, x, y) in got:
+    for (tok, x, y) in got[3] + got[0] + got[4] + got[1] + got[5][:1] + got[2][:1] + got[5][1:] + got[2][1:]:
         need("t", tok)
         for c in range(x // 128, y // 128):
             m = mm(T.PV[:, c:c + 1], T.G[:, 128 * c:128 * c + 128], T.SEL[:, 0:1], True, True)
@@ -321,15 +359,18 @@ def rank_program(g, core, T, topo):
     ps = cp(T.PS[:], T.PV[:, 0:48])
 
     tab_tok = []
+
+    def tab_pass(lo, hi):
+        for c in range(lo, hi):
+            need("p", tab_tok[c])
+            blk = T.TAB[:, c * CW:c * CW + CW]
+            send([([own[oi + 1]], bits(topo.mask(core, own[oi + 1])), "ta%d" % c, blk, blk)])
+
     if oi is not None:
         for c in range(NCH):
-            tok = ("tl%d" % c, 16) if is_rank else expect("ta%d" % c, len(bits(topo.mask(own[oi - 1], core))))
-            tab_tok.append(tok)
-            if oi < 2:
-                need("p", tok)
-                blk = T.TAB[:, c * CW:c * CW + CW]
-                send([([own[oi + 1]], bits(topo.mask(core, own[oi + 1])), "ta%d" % c, blk, blk)])
-
+            tab_tok.append(("tl%d" % c, 16) if is_rank else expect("ta%d" % c, len(bits(topo.mask(own[oi - 1], core)))))
+    if oi in (0, 1):
+        tab_pass(0, BEFORE[oi])
     need("p", ps)
     to = [c for c in own if c != core]
     tr = []
@@ -339,9 +380,12 @@ def rank_program(g, core, T, topo):
         tr.append(([d], bits(topo.mask(core, d))[n * j:n * j + n], "pt_arr", T.PS[:, 16 * k:16 * k + 16],
                    T.PT[:, 16 * slot:16 * slot + 16]))
     send(tr)
+    if oi in (0, 1):
+        tab_pass(BEFORE[oi], NCH)
 
     if oi is not None:
         reqs = sets[oi]
+        away = [cores[r] for r in reqs if cores[r] != core]
         need("v", c_ml)
         c_lt = ts(T.LT[:], T.ML[:], PIX, -1.0, OP.is_le, OP.mult)
         a = fill(T.RST[:], 1.0)
@@ -380,34 +424,50 @@ def rank_program(g, core, T, topo):
         need("v", a)
         a = cp(T.KLF[:], T.KLH[:])
         need("p", ff)
-        se = slot_engines(topo, core, [cores[r] for r in reqs if cores[r] != core])
+        se = split_engines(topo, core, away, 4)
         send([([cores[r]], se[cores[r]], "sl_arr", T.F[:, 8 * rr:8 * rr + 8], T.SL[:, 8 * si:8 * si + 8])
               for rr, r in enumerate(reqs) if cores[r] != core])
-        need("v", a)
-        for c in range(16):
-            rr = c // 8
+        need("v", a, c_i128)
+        land = T.L[:, CAPP * (si + 1):CAPP * (si + 2)]
+        PLs = [T.PL, T.PX]
+        own_tok = []
+
+        def onehot(c):
             ts(T.AH[:, 128 * c:128 * c + 128], T.I128[:], T.KLF[:, c:c + 1], None, OP.is_equal)
             b = ts(T.BH[:, 16 * c:16 * c + 16], T.I128[:, 0:16], T.KLF[:, 16 + c:17 + c], T.COL[:, c:c + 1], OP.is_equal, OP.mult)
             need("t", b)
-            m = mm(T.PL[:, 16 * rr:16 * rr + 16], T.AH[:, 128 * c:128 * c + 128], T.BH[:, 16 * c:16 * c + 16], c % 8 == 0, c % 8 == 7)
-        need("v", m)
-        a = ts(T.LST[:], T.PL[:, 0:32], 2048.0, None, OP.add)
-        need("v", a, *tab_tok)
-        for rr, r in enumerate(reqs):
+            return mm(PLs[c // 8][:, 0:16], T.AH[:, 128 * c:128 * c + 128], T.BH[:, 16 * c:16 * c + 16], c % 8 == 0, c % 8 == 7)
+
+        def deliver(rr, q, m):
+            r = reqs[rr]
+            need("v", m)
+            lst = ts(T.LST[:, 16 * rr:16 * rr + 16], PLs[rr][:, 0:16], 2048.0, None, OP.add)
+            need(q, lst, *tab_tok)
             here = cores[r] == core
-            land = T.L[:, CAPP * (si + 1):CAPP * (si + 2)]
             out = land if here else T.DT[:, CAPP * rr:CAPP * rr + CAPP]
-            d = cp(out, T.TAB[:].indirect(T.LST[:, 16 * rr:16 * rr + 16]))
-            if not here:
+            src = T.TAB[:].indirect(T.LST[:, 16 * rr:16 * rr + 16])
+            d = act(out, src) if q == "s" else cp(out, src)
+            if here:
+                own_tok.append(d)
+            else:
                 need("p", d)
                 send([([cores[r]], bits(topo.mask(core, cores[r])), "dt_arr", out, land)])
+
+        for c in range(8):
+            m = onehot(c)
+        onehot(8)
+        deliver(0, "s", m)
+        for c in range(9, 16):
+            m = onehot(c)
+        deliver(1, "v", m)
 
     if is_rank:
         sl_n = dt_n = 0
         for tm in P["teams"]:
             for src, q in zip(tm["own"], tm["sets"]):
                 if si in q and src != core:
-                    sl_n += len(slot_engines(topo, src, [cores[r] for r in q if cores[r] != src])[core])
+                    to = [cores[r] for r in q if cores[r] != src]
+                    sl_n += len(split_engines(topo, src, to, 4)[core])
                     dt_n += len(bits(topo.mask(src, core)))
         need("v", expect("sl_arr", sl_n), ("cv", cnt["cv"]))
         a = tt(T.SA[:, 0:24], T.SL[:, 0:24], T.SL[:, 24:48], OP.add)
@@ -420,11 +480,15 @@ def rank_program(g, core, T, topo):
             m = mm(T.PW[:, b:64:8], T.EH[:, 128 * b:128 * b + 128], T.SA[:, 32:40], True, True)
         need("v", m)
         a = cp(T.SLU[:], T.PW[:, 0:64])
-        need("v", a, expect("dt_arr", dt_n))
-        for h in range(2):
-            yt = cp(T.YT[:, 512 * h:512 * h + 512], T.L[:].indirect(T.SLU[:, 32 * h:32 * h + 32]))
-            need("ys"[h], yt)
-            dma("ys"[h], "st", T.y[:, 512 * h:512 * h + 512], T.YT[:, 512 * h:512 * h + 512])
+        dta = expect("dt_arr", dt_n)
+        need("v", a, dta, *own_tok)
+        need("s", a, dta, *own_tok)
+        v = cp(T.YT[:, 0:512], T.L[:].indirect(T.SLU[:, 0:32]))
+        w = act(T.YT[:, 512:1024], T.L[:].indirect(T.SLU[:, 32:64]))
+        need("y", v)
+        dma("y", "st", T.y[:, 0:512], T.YT[:, 0:512])
+        need("s", w)
+        dma("s", "st", T.y[:, 512:1024], T.YT[:, 512:1024])
 
     for sem in tot:
         need("p", (sem, tot[sem]))

@@ -4,34 +4,38 @@ from concourse.mybir import AluOpType, ActivationFunctionType
 N = 6
 R, T_ENT, CAPP = 4096, 1024, 256
 SIM = 80
-NCH = 4
-N_EARLY = 2
-BEFORE = (4, 2)
+HOME, OUT = (0,), ((1,), (2,))
+NCH = 8
+N_EARLY = 5
+BEFORE = (8, 2)
 CW = R // NCH
-NC_RANK, NC_HELP = 46, 70
-DUMP = 16 * NC_HELP
+NC_RANK, NC_HELP, NC_OUT = 52, 68, 64
+DUMP = 128 * NC_HELP
 PADL, TABLE, PADR = 8, 24576, 16
 WALL = DUMP + PADL + TABLE + PADR
 ZS = 2048
+FILL_S = {"rank": (6, 2, 0), "help": (5, 2, 0), "out": (4, 3, 0)}
+FILL_D = {"rank": 0, "help": 2, "out": 2}
+FILL_G = {"rank": 0, "help": 1024, "out": 1024}
 
 _COLS = {
-    "int32": {"KA": 64, "KAI": 192, "KBR": 256, "KB": NC_HELP, "KBI": 2 * NC_HELP, "PI": 4, "KI": 16, "KLH": 32},
-    "float32": {"KBE": NC_HELP, "KBT": NC_HELP, "CF": 4, "CM": 6, "P16": 8, "JN": NC_HELP, "J": NC_HELP, "C1": NC_HELP, "HQ": 8,
-                "RST": 16, "PS": 48, "PT": 48, "T1": 32, "VV": 16, "PEN": 16, "COL": 16, "KLF": 32, "FT": 16},
-    "bfloat16": {"X": 192, "W": WALL, "V": 16 * NC_HELP, "G": N * T_ENT, "LI": 256, "SEL": 2, "I128": 128, "ML": 128,
-                 "BIAS": 256, "ONE": 128, "E": 768, "LT": 128, "MM": 16, "CUM": 16, "TAB": R, "DT": 2 * CAPP,
+    "int32": {"KA": 64, "KBR": 256, "KB": NC_HELP, "PI": 4, "KI": 16, "KLH": 32},
+    "float32": {"KBX": 4 * NC_HELP, "CM": 6, "P16": 8, "J": NC_HELP, "HQ": 8, "RST": 16, "PS": 48, "PT": 64, "OW": 80,
+                "COL": 16, "X": 64, "E": 768, "WT": 8, "GB": 8, "PIX": 4},
+    "bfloat16": {"W": WALL, "V": 16 * NC_HELP, "G": N * T_ENT, "LI": 256, "SEL": 2, "I128": 128, "ML": 128,
+                 "BIAS": 256, "ONE": 128, "LT": 128, "MM": 16, "CUM": 16, "TAB": R, "DT": 2 * CAPP,
                  "L": CAPP * (N + 1), "YT": T_ENT},
-    "float16": {"EH": 1024, "F": 16, "AH": 2048, "BH": 256, "SL": 8 * N, "SA": 40},
-    "uint16": {"OFB": NC_HELP, "OFQ": 384, "LST": 32, "SLU": 64},
+    "float16": {"EH": 1024, "F": 16, "AH": 256, "BQ": 256, "BH": 256, "LS": 32, "REP": 128, "SL": 8 * N, "SA": 40},
+    "uint16": {"OFB": NC_HELP, "OFQ": 384, "LST": 32, "SLU": 64, "OX": 16},
 }
-SCRATCH = {"kaq": ("dram", [N, 128, 8], "int32")}
+SCRATCH = {"kaq": ("dram", [N, 128, 8], "int32"), "kbd": ("dram", [4, 128, 8], "int32")}
 for _d in _COLS:
     for _n in _COLS[_d]:
         SCRATCH[_n] = ("sbuf", [128, _COLS[_d][_n]], _d)
 for _n in ("PQ0", "PQ1", "PX", "PV", "PK", "PL", "PW"):
     SCRATCH[_n] = ("psum", [128, 512], "float32")
-SEMAPHORES = ["ld_a", "ld_b", "ka_arr", "ka_rel", "ka_ld", "kb_arr", "go", "fz", "pt_arr", "sl_arr", "dt_arr", "st", "loc",
-              "cv", "cs", "cp", "ct"] + ["tl%d" % c for c in range(NCH)] + ["ta%d" % c for c in range(NCH)]
+SEMAPHORES = ["ld_a", "ld_b", "ld_k", "ka_arr", "ka_rel", "ka_ld", "kb_arr", "go", "fz", "pt_arr", "sl_arr", "dt_arr", "st",
+              "loc", "cv", "cs", "cp", "ct"] + ["tl%d" % c for c in range(NCH)] + ["ta%d" % c for c in range(NCH)]
 _PLAN = {}
 
 
@@ -70,39 +74,86 @@ def make_plan(cores, topo):
                 return 0 if cores[r] != s else -1
             return 1 if (topo.mates(a, b) or topo.same_plane(a, b)) else 2
         teams.append({"s": s, "team": team, "own": list(best[1]), "sets": [sorted(q, key=lambda r: -far(r)) for q in best[2]]})
-    everyone = [c for t in teams for c in t["team"]]
+    groups = [(k, teams[k]["team"], HOME) for k in range(N)]
+    taken = set(c for t in teams for c in t["team"])
+    busy = set(topo.chip(c) for c in taken)
+    chips = sorted(set(topo.chip(c) for c in range(SIM)) - busy)
+
+    def choices(k, serve):
+        t, res = teams[k], []
+        for ch in chips:
+            c4 = [c for c in range(SIM) if topo.chip(c) == ch and c not in taken and topo.may_write(t["s"], c)
+                  and all(topo.may_write(c, t["own"][o]) for o in serve)]
+            near = topo.mates(ch, topo.chip(t["s"])) or topo.same_plane(ch, topo.chip(t["s"]))
+            dies = [[c for c in c4 if topo.die(c) == d] for d in (0, 1)]
+            full = [q for q in dies if len(q) == 4]
+            if full:
+                res.append(((0 if near else 1, 0, ch), full[0]))
+            elif len(c4) >= 4:
+                res.append(((0 if near else 1, 1, ch), c4[:4]))
+        return sorted(res)
+
+    todo = [(k, serve) for serve in OUT for k in range(N)]
+    while todo:
+        opts = sorted((sum(1 for x in choices(k, serve) if x[0][0] == 0), todo.index((k, serve))) for k, serve in todo)
+        k, serve = todo.pop(opts[0][1])
+        quad = choices(k, serve)[0][1]
+        taken.update(quad)
+        groups.append((k, quad, serve))
+    pos = {}
+    for (k, mem, serve) in groups:
+        for c in mem:
+            pos[c] = [r for o in serve for r in teams[k]["sets"][o]]
+    everyone = [c for gr in groups for c in gr[1]]
     ka = {c: [] for c in everyone}
     for r in range(N):
         s, t = cores[r], teams[r]
-        mates = t["team"][1:]
-        near = [d for d in everyone if d not in t["team"] and topo.chip(d) == topo.chip(s)]
-        away = [d for d in everyone if topo.chip(d) != topo.chip(s)]
+        near = [d for d in everyone if d not in t["team"] and topo.chip(d) == topo.chip(s) and r in pos[d]]
+        away = [d for d in everyone if topo.chip(d) != topo.chip(s) and r in pos[d]]
         direct = [d for d in away if topo.may_write(s, d)]
         rest = [d for d in away if d not in direct]
         off = bits(topo.mask(s, away[0]))
-        eng = [e for e in bits(topo.mask(s, mates[0])) if e not in off][:4]
-        call = [(r, mates, eng, "ka_rel")]
-        if direct:
-            call.append((r, direct, off, "ka_arr"))
-        ka[s].insert(0, call)
-        third = [c for c in t["team"] if c not in t["own"]]
+        first, ring = [], []
+        for (k, mem, serve) in groups:
+            if serve != HOME and r in pos[mem[0]] and all(d in direct for d in mem):
+                a = 2 * (pos[mem[0]].index(r) % 2)
+                first += mem[a:a + 2]
+                ring += [(mem[a], mem[2 - a]), (mem[a + 1], mem[3 - a])]
+                direct = [d for d in direct if d not in mem]
+        relay = []
         if rest:
             ports = [c for c in t["own"][1:] if all(topo.may_write(c, d) for d in rest)]
             for k, c in enumerate(ports):
-                ka[c].append([(r, rest[k::len(ports)], bits(topo.mask(c, rest[0])), "ka_arr")])
-        third.append(t["own"][2])
-        for k, c in enumerate(third):
-            eng = bits(topo.mask(c, near[0]))
-            if ka[c]:
+                relay.append((c, rest[k::len(ports)], True))
+        third = [c for c in t["team"] if c not in t["own"]] + [t["own"][2]]
+        if near:
+            for k, c in enumerate(third):
+                relay.append((c, near[k::len(third)], False))
+        mates = [c for c in t["team"][1:] if r in pos[c] or c in [x[0] for x in relay]]
+        call = []
+        if mates:
+            eng = [e for e in bits(topo.mask(s, mates[0])) if e not in off][:4]
+            call.append((r, mates, eng, "ka_rel"))
+        oe = off if not (first and direct) else None
+        if direct:
+            call.append((r, direct, oe or off[:len(off) // 2], "ka_arr"))
+        if first:
+            call.append((r, first, oe or off[len(off) // 2:], "ka_rel"))
+        ka[s].insert(0, call)
+        for (c, dsts, far_) in relay:
+            eng = bits(topo.mask(c, dsts[0]))
+            if not far_ and ka[c]:
                 eng = [e for e in eng if e not in off]
-            ka[c].append([(r, near[k::len(third)], eng, "ka_arr")])
+            ka[c].append([(r, dsts, eng, "ka_arr")])
+        for (c, d) in ring:
+            ka[c].append([(r, [d], bits(topo.mask(c, d)), "ka_arr")])
     total = {}
     for c in ka:
         for call in ka[c]:
             for (r, dsts, eng, sem) in call:
                 for d in dsts:
                     total[(d, sem)] = total.get((d, sem), 0) + len(eng)
-    _PLAN.update({"teams": teams, "everyone": everyone, "ka": ka, "katotal": total})
+    _PLAN.update({"teams": teams, "everyone": everyone, "ka": ka, "katotal": total, "groups": groups, "pos": pos})
     return _PLAN
 
 
@@ -118,21 +169,35 @@ def split_engines(topo, src, dsts, most):
     return {dsts[0]: a[:most], dsts[1]: b[:most]}
 
 
+def lookup_engines(topo, src, dsts):
+    res = {}
+    for j, d in enumerate(dsts):
+        e = bits(topo.mask(src, d))
+        n = len(e) // (1, 2, 4)[len(dsts) - 1]
+        res[d] = e[n * j:n * j + n]
+    return res
+
+
 def rank_program(g, core, T, topo):
     cores = list(T.cores)
     P = make_plan(cores, topo)
     if core not in P["everyone"]:
         return
     OP, COPY = AluOpType, ActivationFunctionType.Copy
-    si = [k for k in range(N) if core in P["teams"][k]["team"]][0]
+    si, mem, serve = [gr for gr in P["groups"] if core in gr[1]][0]
     t_ = P["teams"][si]
-    s, own, sets, team = t_["s"], t_["own"], t_["sets"], t_["team"]
-    mi = team.index(core)
+    s, own, sets = t_["s"], t_["own"], t_["sets"]
+    mi = mem.index(core)
     is_rank = core == s
-    nc = NC_RANK if is_rank else NC_HELP
-    c0 = 0 if is_rank else NC_RANK + NC_HELP * (mi - 1)
+    kind = "rank" if is_rank else "help" if serve == HOME else "out"
+    nc = {"rank": NC_RANK, "help": NC_HELP, "out": NC_OUT}[kind]
+    c0 = {"rank": 0, "help": NC_RANK + NC_HELP * (mi - 1), "out": NC_OUT * mi}[kind]
     oi = own.index(core) if core in own else None
-    pos = [r for q in sets for r in q]
+    pos = P["pos"][core]
+    nq = len(pos)
+
+    def slot(c, r):
+        return P["pos"][c].index(r) if r in P["pos"][c] else N - 1
 
     queue = {"v": g.vector, "s": g.scalar, "p": g, "t": g.tensor, "y": g.sync}
     csem = {"v": "cv", "s": "cs", "p": "cp", "t": "ct"}
@@ -162,13 +227,12 @@ def rank_program(g, core, T, topo):
 
     def send(transfers):
         lst = []
-        for (d, e, sem, src, out) in transfers:
+        for (d, e, sem, src, outs) in transfers:
             ids = []
             for c in d:
                 rid, pid, _ = topo.addr(c)
                 ids.append(DstId(rid=rid, pnc=pid))
-            lst.append(RemoteDMATransfer(dst_ids=ids, dma_engine_mask=emask(e), remote_sem=T.sem[sem], srcs=[src],
-                                         dsts=[out for c in d]))
+            lst.append(RemoteDMATransfer(dst_ids=ids, dma_engine_mask=emask(e), remote_sem=T.sem[sem], srcs=[src], dsts=outs))
             expect("loc", len(e))
         g.remote_dma_fused(lst, local_sem=T.sem.loc)
 
@@ -192,14 +256,18 @@ def rank_program(g, core, T, topo):
     def fill(out, c):
         return did("v", g.vector.memset(out, c))
 
-    def act(out, in_):
-        return did("s", g.scalar.activation(out, in_, COPY, bias=-0.0))
+    def act(out, in_, scale=1.0, bias=-0.0):
+        return did("s", g.scalar.activation(out, in_, COPY, bias=bias, scale=scale))
 
     def mm(out, lhsT, rhs, start, stop):
         return did("t", g.tensor.matmul(out, lhsT, rhs, start, stop))
 
+    outside = [c for gr in P["groups"] if gr[0] == si and gr[2] != HOME for c in gr[1]]
     if is_rank:
-        ld_a = dma("y", "ld_a", T.kaq[si], T.ka[:])
+        ld_a = dma("y", "ld_a", T.kaq[slot(core, si)], T.ka[:])
+        if outside:
+            for k in range(4):
+                ld_k = dma("y", "ld_k", T.kbd[k], T.kb[:, NC_OUT * k:NC_OUT * k + NC_OUT])
         for k in range(8):
             ld_b = dma("y" if k % 2 else "s", "ld_b", T.KBR[16 * k:16 * k + 16, :], T.kb[:])
     z0 = fill(T.W[:, DUMP:DUMP + ZS // 2], 0.0)
@@ -207,81 +275,122 @@ def rank_program(g, core, T, topo):
 
     c_pi = did("p", g.iota(T.PI[:, 3:4], pattern=[[0, 1]], base=0, channel_multiplier=1))
     c_hq = iota(T.HQ[:], [[16, 8]], c0, 0)
-    c_jn = iota(T.JN[:], [[16, NC_HELP]], 0, 0)
     c_li = iota(T.LI[:], [[1, 256]], 1, 0)
+    c_j = iota(T.J[:, 0:nc], [[1, nc]], 0, nc)
+    at = [DUMP + ZS]
+    fills = []
+
+    def matrices():
+        c_bias = iota(T.BIAS[:, 0:128], [[-TABLE, 8], [0, 16]], 0, 0)
+        need("p", c_bias)
+        c_bi = select(T.BIAS[:, 128:256], T.BIAS[:, 0:128], [[0, 128]], OP.is_equal, 0.0, 0, 1)
+        need("p", c_bi)
+        c_bi = select(T.BIAS[:, 128:256], T.BIAS[:, 128:256], [[0, 128]], OP.not_equal, float(PADL), -1, 1)
+        need("p", z0)
+        c_wt = select(T.WT[0:16, 0:1], T.W[0:16, DUMP:DUMP + 1], [[0, 1]], OP.not_equal, 16.0, 0, 1)
+        need("p", c_wt)
+        c_wt = select(T.WT[0:16, 0:1], T.WT[0:16, 0:1], [[0, 1]], OP.not_equal, 1.0, -8, 1)
+        c_e = select(T.E[0:16 * nq, 0:128 * nq], T.W[0:16 * nq, DUMP:DUMP + 128 * nq], [[-16, nq], [0, 8], [-1, 16]],
+                     OP.not_equal, 1.0, 0, 1)
+        fills.append(c_e)
+        return c_bi, c_e
+
+    if not is_rank:
+        c_bi, c_e = matrices()
     for n, call in enumerate(P["ka"][core]):
         need("p", ld_a if is_rank and n == 0 else ("ka_rel", P["katotal"][(core, "ka_rel")]))
-        send([(d, e, sem, T.kaq[r], T.kaq[r]) for (r, d, e, sem) in call])
+        send([(d, e, sem, T.kaq[slot(core, r)], [T.kaq[slot(c, r)] for c in d]) for (r, d, e, sem) in call])
     tk = [expect(sem, P["katotal"][(core, sem)]) for sem in ("ka_arr", "ka_rel") if (core, sem) in P["katotal"]]
-    on = bits(topo.mask(s, team[1]))
+    on = bits(topo.mask(s, t_["team"][1]))
     kb_eng = [None, on[:8], on[8:12], on[12:]]
+    kb_out = [bits(topo.mask(s, outside[0]))[2 * k:2 * k + 2] for k in range(4)] if outside else []
     if is_rank:
+        if outside:
+            need("p", ld_k)
+            send([(outside[k::4], kb_out[k], "kb_arr", T.kbd[k], [T.kbd[0] for c in outside[k::4]]) for k in range(4)])
         need("p", ld_b)
-        send([([team[i]], kb_eng[i], "kb_arr", T.KBR[:, NC_RANK + NC_HELP * (i - 1):NC_RANK + NC_HELP * i], T.KB[:])
+        send([([mem[i]], kb_eng[i], "kb_arr", T.KBR[:, NC_RANK + NC_HELP * (i - 1):NC_RANK + NC_HELP * i], [T.KB[:]])
               for i in range(1, 4)])
         g.sem_inc(T.sem.go, 1)
         go = expect("go", 1)
         kb_tok, KB = ld_b, T.KBR[:, 0:nc]
-    else:
+        c_bi, c_e = matrices()
+    elif kind == "help":
         kb_tok, KB = expect("kb_arr", len(kb_eng[mi])), T.KB[:]
-    c_bias = iota(T.BIAS[:, 0:128], [[-32768, 8], [0, 16]], 0, 0)
-    need("p", z0)
-    c_e = select(T.E[0:96, :], T.W[0:96, DUMP:DUMP + 768], [[-16, 6], [0, 8], [-1, 16]], OP.not_equal, 1.0, 0, 1)
-    need("p", c_bias)
-    c_bi = select(T.BIAS[:, 128:256], T.BIAS[:, 0:128], [[0, 128]], OP.is_equal, 0.0, 0, 1)
-    need("p", c_bi)
-    c_bi = select(T.BIAS[:, 128:256], T.BIAS[:, 128:256], [[0, 128]], OP.not_equal, float(PADL), -1, 1)
+    else:
+        kbd = expect("kb_arr", len(kb_out[mi]))
+    if FILL_G[kind]:
+        fills.append(iota(T.W[:, at[0]:at[0] + FILL_G[kind]], [[0, FILL_G[kind]]], 0, 0))
+        at[0] += FILL_G[kind]
     if oi is not None:
         c_i128 = iota(T.I128[:], [[0, 8], [1, 16]], 0, 0)
-        c_p16 = iota(T.P16[:], [[-16, 8]], 0, 1)
+        iota(T.P16[:], [[-16, 8]], 0, 1)
+        iota(T.PIX[:, 0:1], [[0, 1]], 0, 1)
         c_ml = iota(T.ML[:], [[1, 128]], 0, 0)
 
-    w_s, n_d = ([1024] * 8 + [512], 0) if is_rank else ([1024] * 7, 2)
-    at = DUMP + ZS
-    fills = [c_e]
-    need("s", z0)
-    for w in w_s:
-        fills.append(act(T.W[:, at:at + w], T.W[:, DUMP:DUMP + w]))
-        at += w
-    for k in range(n_d):
+    def scalar_fill(w):
+        need("s", z0)
+        fills.append(act(T.W[:, at[0]:at[0] + w], T.W[:, DUMP:DUMP + w]))
+        at[0] += w
+
+    for k in range(FILL_D[kind]):
         need("y", z1)
-        fz = dma("y", "fz", T.W[:, at:at + ZS], T.W[:, DUMP:DUMP + ZS])
-        at += ZS
-    if n_d:
-        fills.append(fz)
+        fz = dma("y", "fz", T.W[:, at[0]:at[0] + ZS], T.W[:, DUMP:DUMP + ZS])
+        at[0] += ZS
+    if kind == "out":
+        need("y", kbd)
+        for k in range(8):
+            ld_b = dma("y", "ld_b", T.KB[16 * k:16 * k + 16, 0:NC_OUT], T.kbd[0])
+        kb_tok, KB = ld_b, T.KB[:, 0:nc]
+    f1, f2, f3 = FILL_S[kind]
+    for k in range(f1):
+        scalar_fill(1024)
+    c_one = fill(T.ONE[:], 1.0)
+    PQ = [T.PQ0, T.PQ1, T.PX, T.PK, T.PL, T.PW]
+    h = nq // 2
+    ORDER = [k for x in zip(range(h, nq), range(h)) for k in x]
+    need("t", c_one, c_bi)
+    gb = mm(T.PV[:, 48:49], T.BIAS[0:96, 128:256], T.ONE[0:96, 0:1], True, True)
+    for k in ORDER:
+        mm(PQ[k][:, 0:64], T.BIAS[0:96, 128:256], T.ONE[0:96, 0:64], True, False)
+    need("s", gb)
+    act(T.GB[:, 0:1], T.PV[:, 48:49], -1.0, float(PADL))
+    act(T.GB[:, 1:2], T.PV[:, 48:49], -1.0, float(PADL + TABLE - 1))
+    c_gb = act(T.GB[:, 2:3], T.PV[:, 48:49], 1.0, float(DUMP))
+    for k in range(f2):
+        scalar_fill(1024)
+    if f3:
+        scalar_fill(f3)
+    need("t", c_e, c_gb)
+    m = mm(T.PV[:, 49:50], T.E[0:16, 0:128], T.WT[0:16, 0:1], True, True)
+    need("s", m)
+    c_sel = act(T.SEL[:, 0:1], T.PV[:, 49:50])
 
     need("v", c_pi)
-    ts(T.PI[:, 0:1], T.PI[:, 3:4], 15, None, OP.bitwise_and)
-    ts(T.PI[:, 1:2], T.PI[:, 3:4], 4, None, OP.logical_shift_right)
     a = ts(T.PI[:, 2:3], T.PI[:, 3:4], 8, None, OP.bitwise_and)
     need("v", a)
-    cf = cp(T.CF[:], T.PI[:])
-    Q16, GRP, Q8, PIX = T.CF[:, 0:1], T.CF[:, 1:2], T.CF[:, 2:3], T.CF[:, 3:4]
-    need("v", cf)
-    ts(T.CM[:, 0:1], Q8, 0.125, None, OP.mult)
-    a = ts(T.CM[:, 1:2], Q8, -0.125, 1.0, OP.mult, OP.add)
-    need("v", a, c_jn, c_hq)
-    ts(T.J[:], T.JN[:], Q16, None, OP.add)
+    ts(T.CM[:, 0:1], T.PI[:, 2:3], 0.125, None, OP.mult)
+    a = ts(T.CM[:, 1:2], T.PI[:, 2:3], -0.125, 1.0, OP.mult, OP.add)
+    need("v", a, c_hq)
     a = ts(T.HQ[:], T.HQ[:], T.CM[:, 1:2], None, OP.mult)
     need("v", a, c_li)
-    ts(T.C1[:], T.J[:], -1.0, float(DUMP + PADL), OP.mult, OP.add)
     for k in range((nc + 15) // 16):
         w = min(256, 16 * nc - 256 * k)
         ts(T.V[:, 256 * k:256 * k + w], T.LI[:, 0:w], T.CM[:, 0:1], T.HQ[:, k:k + 1], OP.mult, OP.add)
-    c_one = fill(T.ONE[:], 1.0)
-    fill(T.W[:, at:WALL], 0.0)
+    fill(T.W[:, at[0]:WALL], 0.0)
+    if FILL_D[kind]:
+        fills.append(fz)
 
-    need("v", kb_tok)
-    k7, k3, e, t, j = T.KBI[:, 0:nc], T.KBI[:, NC_HELP:NC_HELP + nc], T.KBE[:, 0:nc], T.KBT[:, 0:nc], T.J[:, 0:nc]
-    ts(k7, KB, 7, None, OP.bitwise_and)
-    a = ts(k3, KB, 3, None, OP.logical_shift_right)
+    need("v", kb_tok, c_gb, c_j)
+    e, t, w, u = [T.KBX[:, NC_HELP * k:NC_HELP * k + nc] for k in range(4)]
+    a = ts(w, KB, T.GB[:, 0:1], T.GB[:, 1:2], OP.max, OP.min)
+    b = ts(u, KB, T.GB[:, 2:3], None, OP.add)
     need("v", a)
-    ts(e, k7, GRP, None, OP.is_equal)
-    a = tt(t, k3, T.C1[:, 0:nc], OP.add)
+    a = tt(e, w, KB, OP.is_equal)
+    need("v", a, b)
+    a = tt(t, e, u, OP.mult)
     need("v", a)
-    a = tt(t, e, t, OP.mult)
-    need("v", a)
-    a = tt(t, t, j, OP.add)
+    a = tt(t, t, T.J[:, 0:nc], OP.max)
     need("v", a)
     a = cp(T.OFB[:, 0:nc], t)
     need("v", a, *fills)
@@ -296,39 +405,25 @@ def rank_program(g, core, T, topo):
         tab_load(0, N_EARLY)
         need("y", ld_a)
     need("y", *tk)
-    ka_ld = dma("y", "ka_ld", T.KA[0:96, :], T.kaq[:])
+    ka_ld = dma("y", "ka_ld", T.KA[0:16 * nq, :], T.kaq[0:nq])
     if is_rank:
         tab_load(N_EARLY, NCH)
-    need("t", c_one, c_bi)
-    PQ = [T.PQ0, T.PQ1, T.PX, T.PK, T.PL, T.PW]
-    ORDER = (3, 0, 4, 5, 1, 2)
-    for k in ORDER:
-        mm(PQ[k][:, 0:64], T.BIAS[0:96, 128:256], T.ONE[0:96, 0:64], True, False)
     need("v", ka_ld)
-    ts(T.KAI[0:96, 0:64], T.KA[0:96, :], 7, None, OP.bitwise_and)
-    ts(T.KAI[0:96, 64:128], T.KA[0:96, :], 11, None, OP.logical_shift_right)
-    a = ts(T.KAI[0:96, 128:192], T.KA[0:96, :], 3, 255, OP.logical_shift_right, OP.bitwise_and)
-    need("v", a)
-    ts(T.X[0:96, 0:64], T.KAI[0:96, 0:64], 32768.0, None, OP.mult)
-    ts(T.X[0:96, 64:128], T.KAI[0:96, 64:128], 256.0, None, OP.mult)
-    a = cp(T.X[0:96, 128:192], T.KAI[0:96, 128:192])
-    need("t", a, c_e)
+    a = cp(T.X[0:16 * nq, :], T.KA[0:16 * nq, :])
+    need("t", a)
     spread = {}
     for k in ORDER:
-        r = pos[k]
-        for x in range(3):
-            spread[k] = mm(PQ[k][:, 0:64], T.E[0:96, 128 * r:128 * r + 128], T.X[0:96, 64 * x:64 * x + 64], False, x == 2)
-    ts(T.CM[:, 3:4], Q16, 0.0, 16.0, OP.is_equal, OP.mult)
-    a = ts(T.CM[:, 4:5], Q16, 8.0, None, OP.is_equal)
-    need("v", a)
-    c_sel = tt(T.SEL[:, 0:1], T.CM[:, 3:4], T.CM[:, 4:5], OP.add)
+        spread[k] = mm(PQ[k][:, 0:64], T.E[0:16 * nq, 128 * k:128 * k + 128], T.X[0:16 * nq, :], False, True)
 
-    def offsets(k):
-        need("v", spread[k])
-        return ts(T.OFQ[:, 64 * k:64 * k + 64], PQ[k][:, 0:64], 0.0, float(PADL + TABLE), OP.max, OP.min)
+    off_tok, got = {}, {}
+
+    def offsets(*ks):
+        for k in ks:
+            if k < nq and k not in off_tok:
+                need("v", spread[k])
+                off_tok[k] = ts(T.OFQ[:, 64 * k:64 * k + 64], PQ[k][:, 0:64], 0.0, float(PADL + TABLE), OP.max, OP.min)
 
     TBL = T.W[:, DUMP:WALL]
-    off_tok, got = {}, {}
 
     def look(q, k, parts):
         got[k] = []
@@ -339,24 +434,27 @@ def rank_program(g, core, T, topo):
             tok = act(T.G[:, x:x + n], TBL.indirect(o)) if q == "s" else cp(T.G[:, x:x + n], TBL.indirect(o))
             got[k].append((tok, x, x + n))
 
-    for k in (3, 0, 4):
-        off_tok[k] = offsets(k)
-    look("v", 0, 1)
-    for k in (5, 1):
-        off_tok[k] = offsets(k)
-    look("v", 1, 1)
-    off_tok[2] = offsets(2)
-    look("v", 2, 2)
-    look("s", 3, 1)
-    look("s", 4, 1)
-    look("s", 5, 2)
+    offsets(h, 0, h + 1 if h > 1 else nq)
+    for k in range(h):
+        offsets(k)
+        look("v", k, 2 if k == h - 1 else 1)
+        offsets(h + k + 2)
+        if k + 1 < h:
+            offsets(k + 1)
+    for k in range(h):
+        look("s", h + k, 2 if k == h - 1 else 1)
+    chunks = []
+    for k in range(h - 1):
+        chunks += got[h + k] + got[k]
+    for x in range(2):
+        chunks += [got[nq - 1][x], got[h - 1][x]]
     need("t", c_sel)
-    for (tok, x, y) in got[3] + got[0] + got[4] + got[1] + got[5][:1] + got[2][:1] + got[5][1:] + got[2][1:]:
+    for (tok, x, y) in chunks:
         need("t", tok)
         for c in range(x // 128, y // 128):
             m = mm(T.PV[:, c:c + 1], T.G[:, 128 * c:128 * c + 128], T.SEL[:, 0:1], True, True)
     need("v", m)
-    ps = cp(T.PS[:], T.PV[:, 0:48])
+    ps = cp(T.PS[:, 0:8 * nq], T.PV[:, 0:8 * nq])
 
     tab_tok = []
 
@@ -364,84 +462,105 @@ def rank_program(g, core, T, topo):
         for c in range(lo, hi):
             need("p", tab_tok[c])
             blk = T.TAB[:, c * CW:c * CW + CW]
-            send([([own[oi + 1]], bits(topo.mask(core, own[oi + 1])), "ta%d" % c, blk, blk)])
+            send([([own[oi + 1]], bits(topo.mask(core, own[oi + 1])), "ta%d" % c, blk, [blk])])
 
     if oi is not None:
         for c in range(NCH):
             tab_tok.append(("tl%d" % c, 16) if is_rank else expect("ta%d" % c, len(bits(topo.mask(own[oi - 1], core)))))
     if oi in (0, 1):
         tab_pass(0, BEFORE[oi])
-    need("p", ps)
-    to = [c for c in own if c != core]
-    tr = []
-    for j, d in enumerate(to):
-        n = 8 if len(to) == 2 else 4
-        k, slot = own.index(d), [c for c in team if c != d].index(core)
-        tr.append(([d], bits(topo.mask(core, d))[n * j:n * j + n], "pt_arr", T.PS[:, 16 * k:16 * k + 16],
-                   T.PT[:, 16 * slot:16 * slot + 16]))
-    send(tr)
+
+    def served(c):
+        return [own[o] for o in serve if own[o] != c]
+
+    if served(core):
+        need("p", ps)
+        le = lookup_engines(topo, core, served(core))
+        tr = []
+        for k, o in enumerate(serve):
+            d = own[o]
+            if d != core:
+                place = 16 * [c for c in mem if c != d].index(core)
+                tr.append(([d], le[d], "pt_arr", T.PS[:, 16 * k:16 * k + 16], [T.PT[:, place:place + 16]]))
+        send(tr)
     if oi in (0, 1):
         tab_pass(BEFORE[oi], NCH)
 
     if oi is not None:
         reqs = sets[oi]
         away = [cores[r] for r in reqs if cores[r] != core]
+        T1, VV, PEN, FT = T.OW[:, 0:32], T.OW[:, 32:48], T.OW[:, 48:64], T.OW[:, 64:80]
         need("v", c_ml)
-        c_lt = ts(T.LT[:], T.ML[:], PIX, -1.0, OP.is_le, OP.mult)
+        c_lt = ts(T.LT[:], T.ML[:], T.PIX[:, 0:1], -1.0, OP.is_le, OP.mult)
         a = fill(T.RST[:], 1.0)
-        need("v", a)
+        need("v", a, c_e)
         for rr in range(2):
             fill(T.RST[:, 8 * rr:8 * rr + 1], 0.0)
+        cp(T.REP[0:16, :], T.E[0:16, 0:128])
+        ts(T.OX[:], T.LI[:, 0:16], -1.0, None, OP.add)
         if is_rank:
             fill(T.L[:, 0:CAPP], 0.0)
             for b in range(8):
                 ts(T.EH[:, 128 * b:128 * b + 128], T.I128[:], T.P16[:, b:b + 1], None, OP.is_equal)
-        need("v", ("cv", cnt["cv"]), expect("pt_arr", sum(8 if c in own else 4 for c in team if c != core)))
-        tt(T.T1[:, 0:16], T.PT[:, 0:16], T.PT[:, 16:32], OP.add)
-        a = tt(T.T1[:, 16:32], T.PT[:, 32:48], T.PS[:, 16 * oi:16 * oi + 16], OP.add)
+        gm, gs = [(gr[1], gr[2]) for gr in P["groups"] if gr[0] == si and oi in gr[2]][0]
+        pt_n = sum(len(lookup_engines(topo, c, [own[o] for o in gs if own[o] != c])[core]) for c in gm if c != core)
+        k = gs.index(oi)
+        last = T.PS[:, 16 * k:16 * k + 16] if core in gm else T.PT[:, 48:64]
+        need("v", ("cv", cnt["cv"]), expect("pt_arr", pt_n))
+        tt(T1[:, 0:16], T.PT[:, 0:16], T.PT[:, 16:32], OP.add)
+        a = tt(T1[:, 16:32], T.PT[:, 32:48], last, OP.add)
         need("v", a)
-        a = tt(T.VV[:], T.T1[:, 0:16], T.T1[:, 16:32], OP.add)
+        a = tt(VV, T1[:, 0:16], T1[:, 16:32], OP.add)
         need("v", a)
-        hit = ts(T.MM[:], T.VV[:], 0.5, None, OP.is_ge)
+        hit = ts(T.MM[:], VV, 0.5, None, OP.is_ge)
         need("v", hit)
         cum = did("v", g.vector.tensor_tensor_scan(T.CUM[:], T.RST[:], T.MM[:], 0.0, OP.mult, OP.add))
-        ts(T.PEN[:], T.VV[:], 0.5, 4096.0, OP.is_lt, OP.mult)
-        col = ts(T.COL[:], T.VV[:], -2049.0, None, OP.add)
+        ts(PEN, VV, 0.5, 4096.0, OP.is_lt, OP.mult)
+        col = ts(T.COL[:], VV, -2049.0, None, OP.add)
         need("t", c_lt, hit)
         mm(T.PK[:, 0:16], T.LT[:], T.MM[:], True, False)
         need("t", cum)
         pk = mm(T.PK[:, 0:16], T.ONE[:, 0:128], T.CUM[:], False, True)
         need("v", pk, col)
-        a = tt(T.KI[:], T.PK[:, 0:16], T.PEN[:], OP.add)
-        ft = ts(T.FT[:], T.PK[:, 0:16], float(CAPP * (si + 1)), None, OP.add)
+        a = tt(T.KI[:], T.PK[:, 0:16], PEN, OP.add)
+        need("s", a)
+        ft = act(FT, T.PK[:, 0:16], 1.0, float(CAPP * (si + 1)))
         need("v", a)
-        ts(T.KLH[:, 0:16], T.KI[:], 15, None, OP.bitwise_and)
-        a = ts(T.KLH[:, 16:32], T.KI[:], 4, None, OP.logical_shift_right)
-        need("v", ft)
-        for rr, r in enumerate(reqs):
-            out = T.SL[:, 8 * si:8 * si + 8] if cores[r] == core else T.F[:, 8 * rr:8 * rr + 8]
-            ff = tt(out, T.FT[:, 8 * rr:8 * rr + 8], T.MM[:, 8 * rr:8 * rr + 8], OP.mult)
-        need("v", a)
-        a = cp(T.KLF[:], T.KLH[:])
-        need("p", ff)
-        se = split_engines(topo, core, away, 4)
-        send([([cores[r]], se[cores[r]], "sl_arr", T.F[:, 8 * rr:8 * rr + 8], T.SL[:, 8 * si:8 * si + 8])
-              for rr, r in enumerate(reqs) if cores[r] != core])
-        need("v", a, c_i128)
+        klo = ts(T.KLH[:, 0:16], T.KI[:], 15, None, OP.bitwise_and)
+        khi = ts(T.KLH[:, 16:32], T.KI[:], 4, None, OP.logical_shift_right)
         land = T.L[:, CAPP * (si + 1):CAPP * (si + 2)]
-        PLs = [T.PL, T.PX]
-        own_tok = []
+        PLs, PRs = [T.PL, T.PX], [T.PQ0, T.PQ1]
+        own_tok, lists, rows = [], {}, {}
 
-        def onehot(c):
-            ts(T.AH[:, 128 * c:128 * c + 128], T.I128[:], T.KLF[:, c:c + 1], None, OP.is_equal)
-            b = ts(T.BH[:, 16 * c:16 * c + 16], T.I128[:, 0:16], T.KLF[:, 16 + c:17 + c], T.COL[:, c:c + 1], OP.is_equal, OP.mult)
+        def half(buf, rr):
+            return buf[:, 128 * rr:128 * rr + 128]
+
+        def onehot_a(rr):
+            need("v", klo, c_i128)
+            return tt(half(T.AH, rr), T.KLH[:, 0:16].indirect(T.OX[:, 8 * rr:8 * rr + 8]), T.I128[:], OP.is_equal)
+
+        def onehot_b(rr):
+            need("v", khi)
+            return tt(half(T.BQ, rr), T.KLH[:, 16:32].indirect(T.OX[:, 8 * rr:8 * rr + 8]), T.I128[:], OP.is_equal)
+
+        def onehot_c(rr, b):
+            need("v", b)
+            b = tt(half(T.BH, rr), T.COL[:].indirect(T.OX[:, 8 * rr:8 * rr + 8]), half(T.BQ, rr), OP.mult)
             need("t", b)
-            return mm(PLs[c // 8][:, 0:16], T.AH[:, 128 * c:128 * c + 128], T.BH[:, 16 * c:16 * c + 16], c % 8 == 0, c % 8 == 7)
+            for c in range(8):
+                x = 128 * rr + 16 * c
+                lists[rr] = mm(PLs[rr][0:16, 0:16], T.AH[:, x:x + 16], T.BH[:, x:x + 16], c == 0, c == 7)
 
-        def deliver(rr, q, m):
+        def spread_list(rr):
+            need("v", lists[rr])
+            a = cp(T.LS[0:16, 16 * rr:16 * rr + 16], PLs[rr][0:16, 0:16])
+            need("t", a)
+            rows[rr] = mm(PRs[rr][:, 0:16], T.REP[0:16, :], T.LS[0:16, 16 * rr:16 * rr + 16], True, True)
+
+        def deliver(rr, q):
             r = reqs[rr]
-            need("v", m)
-            lst = ts(T.LST[:, 16 * rr:16 * rr + 16], PLs[rr][:, 0:16], 2048.0, None, OP.add)
+            need("v", rows[rr])
+            lst = ts(T.LST[:, 16 * rr:16 * rr + 16], PRs[rr][:, 0:16], 2048.0, None, OP.add)
             need(q, lst, *tab_tok)
             here = cores[r] == core
             out = land if here else T.DT[:, CAPP * rr:CAPP * rr + CAPP]
@@ -451,15 +570,25 @@ def rank_program(g, core, T, topo):
                 own_tok.append(d)
             else:
                 need("p", d)
-                send([([cores[r]], bits(topo.mask(core, cores[r])), "dt_arr", out, land)])
+                send([([cores[r]], bits(topo.mask(core, cores[r])), "dt_arr", out, [land])])
 
-        for c in range(8):
-            m = onehot(c)
-        onehot(8)
-        deliver(0, "s", m)
-        for c in range(9, 16):
-            m = onehot(c)
-        deliver(1, "v", m)
+        onehot_a(0)
+        onehot_c(0, onehot_b(0))
+        need("v", ft)
+        for rr, r in enumerate(reqs):
+            out = T.SL[:, 8 * si:8 * si + 8] if cores[r] == core else T.F[:, 8 * rr:8 * rr + 8]
+            ff = tt(out, FT[:, 8 * rr:8 * rr + 8], T.MM[:, 8 * rr:8 * rr + 8], OP.mult)
+        need("p", ff)
+        se = split_engines(topo, core, away, 4)
+        send([([cores[r]], se[cores[r]], "sl_arr", T.F[:, 8 * rr:8 * rr + 8], [T.SL[:, 8 * si:8 * si + 8]])
+              for rr, r in enumerate(reqs) if cores[r] != core])
+        spread_list(0)
+        onehot_a(1)
+        b1 = onehot_b(1)
+        deliver(0, "s")
+        onehot_c(1, b1)
+        spread_list(1)
+        deliver(1, "v")
 
     if is_rank:
         sl_n = dt_n = 0
@@ -483,12 +612,11 @@ def rank_program(g, core, T, topo):
         dta = expect("dt_arr", dt_n)
         need("v", a, dta, *own_tok)
         need("s", a, dta, *own_tok)
-        v = cp(T.YT[:, 0:512], T.L[:].indirect(T.SLU[:, 0:32]))
-        w = act(T.YT[:, 512:1024], T.L[:].indirect(T.SLU[:, 32:64]))
-        need("y", v)
-        dma("y", "st", T.y[:, 0:512], T.YT[:, 0:512])
-        need("s", w)
-        dma("s", "st", T.y[:, 512:1024], T.YT[:, 512:1024])
+        v = [cp(T.YT[:, x:x + 256], T.L[:].indirect(T.SLU[:, x // 16:x // 16 + 16])) for x in (0, 256)]
+        w = [act(T.YT[:, x:x + 256], T.L[:].indirect(T.SLU[:, x // 16:x // 16 + 16])) for x in (512, 768)]
+        for q, tok, x in (("y", v[0], 0), ("y", w[0], 512), ("y", v[1], 256), ("s", w[1], 768)):
+            need(q, tok)
+            dma(q, "st", T.y[:, x:x + 256], T.YT[:, x:x + 256])
 
     for sem in tot:
         need("p", (sem, tot[sem]))

from concourse.bass import DstId, RemoteDMATransfer
from concourse.mybir import AluOpType, ActivationFunctionType

N = 6
R, T_ENT, CAPP = 4096, 1024, 256
SIM = 80
HOME, OUT = (0,), ((1,), (2,))
NCH = 8
N_EARLY = 5
BEFORE = (8, 2)
CW = R // NCH
NC_RANK, NC_HELP, NC_OUT = 52, 68, 64
DUMP = 128 * NC_HELP
PADL, TABLE, PADR = 8, 24576, 16
WALL = DUMP + PADL + TABLE + PADR
ZS = 2048
FILL_S = {"rank": (6, 2, 0), "help": (5, 2, 0), "out": (4, 3, 0)}
FILL_D = {"rank": 0, "help": 2, "out": 2}
FILL_G = {"rank": 0, "help": 1024, "out": 1024}

_COLS = {
    "int32": {"KA": 64, "KBR": 256, "KB": NC_HELP, "PI": 4, "KI": 16, "KLH": 32},
    "float32": {"KBX": 4 * NC_HELP, "CM": 6, "P16": 8, "J": NC_HELP, "HQ": 8, "RST": 16, "PS": 48, "PT": 64, "OW": 80,
                "COL": 16, "X": 64, "E": 768, "WT": 8, "GB": 8, "PIX": 4},
    "bfloat16": {"W": WALL, "V": 16 * NC_HELP, "G": N * T_ENT, "LI": 256, "SEL": 2, "I128": 128, "ML": 128,
                 "BIAS": 256, "ONE": 128, "LT": 128, "MM": 16, "CUM": 16, "TAB": R, "DT": 2 * CAPP,
                 "L": CAPP * (N + 1), "YT": T_ENT},
    "float16": {"EH": 1024, "F": 16, "AH": 256, "BQ": 256, "BH": 256, "LS": 32, "REP": 128, "SL": 8 * N, "SA": 40},
    "uint16": {"OFB": NC_HELP, "OFQ": 384, "LST": 32, "SLU": 64, "OX": 16},
}
SCRATCH = {"kaq": ("dram", [N, 128, 8], "int32"), "kbd": ("dram", [4, 128, 8], "int32")}
for _d in _COLS:
    for _n in _COLS[_d]:
        SCRATCH[_n] = ("sbuf", [128, _COLS[_d][_n]], _d)
for _n in ("PQ0", "PQ1", "PX", "PV", "PK", "PL", "PW"):
    SCRATCH[_n] = ("psum", [128, 512], "float32")
SEMAPHORES = ["ld_a", "ld_b", "ld_k", "ka_arr", "ka_rel", "ka_ld", "kb_arr", "go", "fz", "pt_arr", "sl_arr", "dt_arr", "st",
              "loc", "cv", "cs", "cp", "ct"] + ["tl%d" % c for c in range(NCH)] + ["ta%d" % c for c in range(NCH)]
_PLAN = {}


def bits(m):
    return [i for i in range(16) if (m >> i) & 1]


def emask(engines):
    return sum(1 << e for e in engines)


def make_plan(cores, topo):
    if _PLAN:
        return _PLAN
    teams = []
    for s in cores:
        team = [s] + [c for c in range(SIM) if c != s and topo.chip(c) == topo.chip(s) and topo.die(c) == topo.die(s)]
        best = None
        for own in [(s, a, b) for a in team[1:] for b in team[1:] if a != b]:
            may = [[r for r in range(N) if cores[r] == o or topo.may_write(o, cores[r])] for o in own]
            for q0 in [(x, y) for x in may[0] for y in may[0] if x < y]:
                for q1 in [(x, y) for x in may[1] for y in may[1] if x < y and x not in q0 and y not in q0]:
                    q2 = tuple(r for r in range(N) if r not in q0 + q1)
                    if not all(r in may[2] for r in q2):
                        continue
                    sets = (q0, q1, q2)
                    off = [sum(topo.chip(cores[r]) != topo.chip(s) for r in q) for q in sets]
                    same = sum(topo.chip(cores[q[0]]) == topo.chip(cores[q[1]]) for q in sets)
                    cost = (max(off), 0 if cores.index(s) in q0 else 1, off[0], same)
                    if best is None or cost < best[0]:
                        best = (cost, own, sets)

        def far(r):
            a, b = topo.chip(s), topo.chip(cores[r])
            if a == b:
                return 0 if cores[r] != s else -1
            return 1 if (topo.mates(a, b) or topo.same_plane(a, b)) else 2
        teams.append({"s": s, "team": team, "own": list(best[1]), "sets": [sorted(q, key=lambda r: -far(r)) for q in best[2]]})
    groups = [(k, teams[k]["team"], HOME) for k in range(N)]
    taken = set(c for t in teams for c in t["team"])
    busy = set(topo.chip(c) for c in taken)
    chips = sorted(set(topo.chip(c) for c in range(SIM)) - busy)

    def choices(k, serve):
        t, res = teams[k], []
        for ch in chips:
            c4 = [c for c in range(SIM) if topo.chip(c) == ch and c not in taken and topo.may_write(t["s"], c)
                  and all(topo.may_write(c, t["own"][o]) for o in serve)]
            near = topo.mates(ch, topo.chip(t["s"])) or topo.same_plane(ch, topo.chip(t["s"]))
            dies = [[c for c in c4 if topo.die(c) == d] for d in (0, 1)]
            full = [q for q in dies if len(q) == 4]
            if full:
                res.append(((0 if near else 1, 0, ch), full[0]))
            elif len(c4) >= 4:
                res.append(((0 if near else 1, 1, ch), c4[:4]))
        return sorted(res)

    todo = [(k, serve) for serve in OUT for k in range(N)]
    while todo:
        opts = sorted((sum(1 for x in choices(k, serve) if x[0][0] == 0), todo.index((k, serve))) for k, serve in todo)
        k, serve = todo.pop(opts[0][1])
        quad = choices(k, serve)[0][1]
        taken.update(quad)
        groups.append((k, quad, serve))
    pos = {}
    for (k, mem, serve) in groups:
        for c in mem:
            pos[c] = [r for o in serve for r in teams[k]["sets"][o]]
    everyone = [c for gr in groups for c in gr[1]]
    ka = {c: [] for c in everyone}
    for r in range(N):
        s, t = cores[r], teams[r]
        near = [d for d in everyone if d not in t["team"] and topo.chip(d) == topo.chip(s) and r in pos[d]]
        away = [d for d in everyone if topo.chip(d) != topo.chip(s) and r in pos[d]]
        direct = [d for d in away if topo.may_write(s, d)]
        rest = [d for d in away if d not in direct]
        off = bits(topo.mask(s, away[0]))
        first, ring = [], []
        for (k, mem, serve) in groups:
            if serve != HOME and r in pos[mem[0]] and all(d in direct for d in mem):
                a = 2 * (pos[mem[0]].index(r) % 2)
                first += mem[a:a + 2]
                ring += [(mem[a], mem[2 - a]), (mem[a + 1], mem[3 - a])]
                direct = [d for d in direct if d not in mem]
        relay = []
        if rest:
            ports = [c for c in t["own"][1:] if all(topo.may_write(c, d) for d in rest)]
            for k, c in enumerate(ports):
                relay.append((c, rest[k::len(ports)], True))
        third = [c for c in t["team"] if c not in t["own"]] + [t["own"][2]]
        if near:
            for k, c in enumerate(third):
                relay.append((c, near[k::len(third)], False))
        mates = [c for c in t["team"][1:] if r in pos[c] or c in [x[0] for x in relay]]
        call = []
        if mates:
            eng = [e for e in bits(topo.mask(s, mates[0])) if e not in off][:4]
            call.append((r, mates, eng, "ka_rel"))
        oe = off if not (first and direct) else None
        if direct:
            call.append((r, direct, oe or off[:len(off) // 2], "ka_arr"))
        if first:
            call.append((r, first, oe or off[len(off) // 2:], "ka_rel"))
        ka[s].insert(0, call)
        for (c, dsts, far_) in relay:
            eng = bits(topo.mask(c, dsts[0]))
            if not far_ and ka[c]:
                eng = [e for e in eng if e not in off]
            ka[c].append([(r, dsts, eng, "ka_arr")])
        for (c, d) in ring:
            ka[c].append([(r, [d], bits(topo.mask(c, d)), "ka_arr")])
    total = {}
    for c in ka:
        for call in ka[c]:
            for (r, dsts, eng, sem) in call:
                for d in dsts:
                    total[(d, sem)] = total.get((d, sem), 0) + len(eng)
    _PLAN.update({"teams": teams, "everyone": everyone, "ka": ka, "katotal": total, "groups": groups, "pos": pos})
    return _PLAN


def split_engines(topo, src, dsts, most):
    dsts = sorted(dsts, key=lambda c: len(bits(topo.mask(src, c))))
    a = bits(topo.mask(src, dsts[0]))
    if len(dsts) == 1:
        return {dsts[0]: a[:most]}
    b = [e for e in bits(topo.mask(src, dsts[1])) if e not in a]
    if not b:
        h = len(a) // 2
        a, b = a[:h], a[h:]
    return {dsts[0]: a[:most], dsts[1]: b[:most]}


def lookup_engines(topo, src, dsts):
    res = {}
    for j, d in enumerate(dsts):
        e = bits(topo.mask(src, d))
        n = len(e) // (1, 2, 4)[len(dsts) - 1]
        res[d] = e[n * j:n * j + n]
    return res


def rank_program(g, core, T, topo):
    cores = list(T.cores)
    P = make_plan(cores, topo)
    if core not in P["everyone"]:
        return
    OP, COPY = AluOpType, ActivationFunctionType.Copy
    si, mem, serve = [gr for gr in P["groups"] if core in gr[1]][0]
    t_ = P["teams"][si]
    s, own, sets = t_["s"], t_["own"], t_["sets"]
    mi = mem.index(core)
    is_rank = core == s
    kind = "rank" if is_rank else "help" if serve == HOME else "out"
    nc = {"rank": NC_RANK, "help": NC_HELP, "out": NC_OUT}[kind]
    c0 = {"rank": 0, "help": NC_RANK + NC_HELP * (mi - 1), "out": NC_OUT * mi}[kind]
    oi = own.index(core) if core in own else None
    pos = P["pos"][core]
    nq = len(pos)

    def slot(c, r):
        return P["pos"][c].index(r) if r in P["pos"][c] else N - 1

    queue = {"v": g.vector, "s": g.scalar, "p": g, "t": g.tensor, "y": g.sync}
    csem = {"v": "cv", "s": "cs", "p": "cp", "t": "ct"}
    cnt = {"cv": 0, "cs": 0, "cp": 0, "ct": 0}
    tot = {}
    seen = {}

    def need(q, *toks):
        for sem, val in toks:
            if seen.get((q, sem), 0) < val:
                queue[q].wait_ge(T.sem[sem], val)
                seen[(q, sem)] = val

    def did(q, ins):
        sem = csem[q]
        ins.then_inc(T.sem[sem], 1)
        cnt[sem] += 1
        return (sem, cnt[sem])

    def expect(sem, n):
        tot[sem] = tot.get(sem, 0) + n
        return (sem, tot[sem])

    def dma(q, sem, out, in_):
        queue[q].dma_start(out, in_).then_inc(T.sem[sem], 16)
        return expect(sem, 16)

    def send(transfers):
        lst = []
        for (d, e, sem, src, outs) in transfers:
            ids = []
            for c in d:
                rid, pid, _ = topo.addr(c)
                ids.append(DstId(rid=rid, pnc=pid))
            lst.append(RemoteDMATransfer(dst_ids=ids, dma_engine_mask=emask(e), remote_sem=T.sem[sem], srcs=[src], dsts=outs))
            expect("loc", len(e))
        g.remote_dma_fused(lst, local_sem=T.sem.loc)

    def iota(out, pattern, base, cm):
        return did("p", g.iota(out, pattern=pattern, base=base, channel_multiplier=cm, allow_small_or_imprecise_dtypes=True))

    def select(out, in_, pattern, op, fill_, base, cm):
        return did("p", g.affine_select(out, in_, pattern=pattern, compare_op=op, fill=fill_, base=base, channel_multiplier=cm))

    def ts(out, in0, s1, s2, op0, op1=None):
        if op1 is None:
            return did("v", g.vector.tensor_scalar(out, in0, s1, s2, op0))
        return did("v", g.vector.tensor_scalar(out, in0, s1, s2, op0, op1))

    def tt(out, in0, in1, op):
        return did("v", g.vector.tensor_tensor(out, in0, in1, op))

    def cp(out, in_):
        return did("v", g.vector.tensor_copy(out, in_))

    def fill(out, c):
        return did("v", g.vector.memset(out, c))

    def act(out, in_, scale=1.0, bias=-0.0):
        return did("s", g.scalar.activation(out, in_, COPY, bias=bias, scale=scale))

    def mm(out, lhsT, rhs, start, stop):
        return did("t", g.tensor.matmul(out, lhsT, rhs, start, stop))

    outside = [c for gr in P["groups"] if gr[0] == si and gr[2] != HOME for c in gr[1]]
    if is_rank:
        ld_a = dma("y", "ld_a", T.kaq[slot(core, si)], T.ka[:])
        if outside:
            for k in range(4):
                ld_k = dma("y", "ld_k", T.kbd[k], T.kb[:, NC_OUT * k:NC_OUT * k + NC_OUT])
        for k in range(8):
            ld_b = dma("y" if k % 2 else "s", "ld_b", T.KBR[16 * k:16 * k + 16, :], T.kb[:])
    z0 = fill(T.W[:, DUMP:DUMP + ZS // 2], 0.0)
    z1 = fill(T.W[:, DUMP + ZS // 2:DUMP + ZS], 0.0)

    c_pi = did("p", g.iota(T.PI[:, 3:4], pattern=[[0, 1]], base=0, channel_multiplier=1))
    c_hq = iota(T.HQ[:], [[16, 8]], c0, 0)
    c_li = iota(T.LI[:], [[1, 256]], 1, 0)
    c_j = iota(T.J[:, 0:nc], [[1, nc]], 0, nc)
    at = [DUMP + ZS]
    fills = []

    def matrices():
        c_bias = iota(T.BIAS[:, 0:128], [[-TABLE, 8], [0, 16]], 0, 0)
        need("p", c_bias)
        c_bi = select(T.BIAS[:, 128:256], T.BIAS[:, 0:128], [[0, 128]], OP.is_equal, 0.0, 0, 1)
        need("p", c_bi)
        c_bi = select(T.BIAS[:, 128:256], T.BIAS[:, 128:256], [[0, 128]], OP.not_equal, float(PADL), -1, 1)
        need("p", z0)
        c_wt = select(T.WT[0:16, 0:1], T.W[0:16, DUMP:DUMP + 1], [[0, 1]], OP.not_equal, 16.0, 0, 1)
        need("p", c_wt)
        c_wt = select(T.WT[0:16, 0:1], T.WT[0:16, 0:1], [[0, 1]], OP.not_equal, 1.0, -8, 1)
        c_e = select(T.E[0:16 * nq, 0:128 * nq], T.W[0:16 * nq, DUMP:DUMP + 128 * nq], [[-16, nq], [0, 8], [-1, 16]],
                     OP.not_equal, 1.0, 0, 1)
        fills.append(c_e)
        return c_bi, c_e

    if not is_rank:
        c_bi, c_e = matrices()
    for n, call in enumerate(P["ka"][core]):
        need("p", ld_a if is_rank and n == 0 else ("ka_rel", P["katotal"][(core, "ka_rel")]))
        send([(d, e, sem, T.kaq[slot(core, r)], [T.kaq[slot(c, r)] for c in d]) for (r, d, e, sem) in call])
    tk = [expect(sem, P["katotal"][(core, sem)]) for sem in ("ka_arr", "ka_rel") if (core, sem) in P["katotal"]]
    on = bits(topo.mask(s, t_["team"][1]))
    kb_eng = [None, on[:8], on[8:12], on[12:]]
    kb_out = [bits(topo.mask(s, outside[0]))[2 * k:2 * k + 2] for k in range(4)] if outside else []
    if is_rank:
        if outside:
            need("p", ld_k)
            send([(outside[k::4], kb_out[k], "kb_arr", T.kbd[k], [T.kbd[0] for c in outside[k::4]]) for k in range(4)])
        need("p", ld_b)
        send([([mem[i]], kb_eng[i], "kb_arr", T.KBR[:, NC_RANK + NC_HELP * (i - 1):NC_RANK + NC_HELP * i], [T.KB[:]])
              for i in range(1, 4)])
        g.sem_inc(T.sem.go, 1)
        go = expect("go", 1)
        kb_tok, KB = ld_b, T.KBR[:, 0:nc]
        c_bi, c_e = matrices()
    elif kind == "help":
        kb_tok, KB = expect("kb_arr", len(kb_eng[mi])), T.KB[:]
    else:
        kbd = expect("kb_arr", len(kb_out[mi]))
    if FILL_G[kind]:
        fills.append(iota(T.W[:, at[0]:at[0] + FILL_G[kind]], [[0, FILL_G[kind]]], 0, 0))
        at[0] += FILL_G[kind]
    if oi is not None:
        c_i128 = iota(T.I128[:], [[0, 8], [1, 16]], 0, 0)
        iota(T.P16[:], [[-16, 8]], 0, 1)
        iota(T.PIX[:, 0:1], [[0, 1]], 0, 1)
        c_ml = iota(T.ML[:], [[1, 128]], 0, 0)

    def scalar_fill(w):
        need("s", z0)
        fills.append(act(T.W[:, at[0]:at[0] + w], T.W[:, DUMP:DUMP + w]))
        at[0] += w

    for k in range(FILL_D[kind]):
        need("y", z1)
        fz = dma("y", "fz", T.W[:, at[0]:at[0] + ZS], T.W[:, DUMP:DUMP + ZS])
        at[0] += ZS
    if kind == "out":
        need("y", kbd)
        for k in range(8):
            ld_b = dma("y", "ld_b", T.KB[16 * k:16 * k + 16, 0:NC_OUT], T.kbd[0])
        kb_tok, KB = ld_b, T.KB[:, 0:nc]
    f1, f2, f3 = FILL_S[kind]
    for k in range(f1):
        scalar_fill(1024)
    c_one = fill(T.ONE[:], 1.0)
    PQ = [T.PQ0, T.PQ1, T.PX, T.PK, T.PL, T.PW]
    h = nq // 2
    ORDER = [k for x in zip(range(h, nq), range(h)) for k in x]
    need("t", c_one, c_bi)
    gb = mm(T.PV[:, 48:49], T.BIAS[0:96, 128:256], T.ONE[0:96, 0:1], True, True)
    for k in ORDER:
        mm(PQ[k][:, 0:64], T.BIAS[0:96, 128:256], T.ONE[0:96, 0:64], True, False)
    need("s", gb)
    act(T.GB[:, 0:1], T.PV[:, 48:49], -1.0, float(PADL))
    act(T.GB[:, 1:2], T.PV[:, 48:49], -1.0, float(PADL + TABLE - 1))
    c_gb = act(T.GB[:, 2:3], T.PV[:, 48:49], 1.0, float(DUMP))
    for k in range(f2):
        scalar_fill(1024)
    if f3:
        scalar_fill(f3)
    need("t", c_e, c_gb)
    m = mm(T.PV[:, 49:50], T.E[0:16, 0:128], T.WT[0:16, 0:1], True, True)
    need("s", m)
    c_sel = act(T.SEL[:, 0:1], T.PV[:, 49:50])

    need("v", c_pi)
    a = ts(T.PI[:, 2:3], T.PI[:, 3:4], 8, None, OP.bitwise_and)
    need("v", a)
    ts(T.CM[:, 0:1], T.PI[:, 2:3], 0.125, None, OP.mult)
    a = ts(T.CM[:, 1:2], T.PI[:, 2:3], -0.125, 1.0, OP.mult, OP.add)
    need("v", a, c_hq)
    a = ts(T.HQ[:], T.HQ[:], T.CM[:, 1:2], None, OP.mult)
    need("v", a, c_li)
    for k in range((nc + 15) // 16):
        w = min(256, 16 * nc - 256 * k)
        ts(T.V[:, 256 * k:256 * k + w], T.LI[:, 0:w], T.CM[:, 0:1], T.HQ[:, k:k + 1], OP.mult, OP.add)
    fill(T.W[:, at[0]:WALL], 0.0)
    if FILL_D[kind]:
        fills.append(fz)

    need("v", kb_tok, c_gb, c_j)
    e, t, w, u = [T.KBX[:, NC_HELP * k:NC_HELP * k + nc] for k in range(4)]
    a = ts(w, KB, T.GB[:, 0:1], T.GB[:, 1:2], OP.max, OP.min)
    b = ts(u, KB, T.GB[:, 2:3], None, OP.add)
    need("v", a)
    a = tt(e, w, KB, OP.is_equal)
    need("v", a, b)
    a = tt(t, e, u, OP.mult)
    need("v", a)
    a = tt(t, t, T.J[:, 0:nc], OP.max)
    need("v", a)
    a = cp(T.OFB[:, 0:nc], t)
    need("v", a, *fills)
    scat = cp(T.W[:, 0:WALL].indirect(T.OFB[:, 0:nc]), T.V[:, 0:16 * nc])

    def tab_load(lo, hi):
        for c in range(lo, hi):
            dma("y", "tl%d" % c, T.TAB[:, c * CW:c * CW + CW], T.tab[:, c * CW:c * CW + CW])

    if is_rank:
        need("y", go)
        tab_load(0, N_EARLY)
        need("y", ld_a)
    need("y", *tk)
    ka_ld = dma("y", "ka_ld", T.KA[0:16 * nq, :], T.kaq[0:nq])
    if is_rank:
        tab_load(N_EARLY, NCH)
    need("v", ka_ld)
    a = cp(T.X[0:16 * nq, :], T.KA[0:16 * nq, :])
    need("t", a)
    spread = {}
    for k in ORDER:
        spread[k] = mm(PQ[k][:, 0:64], T.E[0:16 * nq, 128 * k:128 * k + 128], T.X[0:16 * nq, :], False, True)

    off_tok, got = {}, {}

    def offsets(*ks):
        for k in ks:
            if k < nq and k not in off_tok:
                need("v", spread[k])
                off_tok[k] = ts(T.OFQ[:, 64 * k:64 * k + 64], PQ[k][:, 0:64], 0.0, float(PADL + TABLE), OP.max, OP.min)

    TBL = T.W[:, DUMP:WALL]

    def look(q, k, parts):
        got[k] = []
        n = T_ENT // parts
        need(q, off_tok[k], scat)
        for x in range(T_ENT * k, T_ENT * k + T_ENT, n):
            o = T.OFQ[:, x // 16:(x + n) // 16]
            tok = act(T.G[:, x:x + n], TBL.indirect(o)) if q == "s" else cp(T.G[:, x:x + n], TBL.indirect(o))
            got[k].append((tok, x, x + n))

    offsets(h, 0, h + 1 if h > 1 else nq)
    for k in range(h):
        offsets(k)
        look("v", k, 2 if k == h - 1 else 1)
        offsets(h + k + 2)
        if k + 1 < h:
            offsets(k + 1)
    for k in range(h):
        look("s", h + k, 2 if k == h - 1 else 1)
    chunks = []
    for k in range(h - 1):
        chunks += got[h + k] + got[k]
    for x in range(2):
        chunks += [got[nq - 1][x], got[h - 1][x]]
    need("t", c_sel)
    for (tok, x, y) in chunks:
        need("t", tok)
        for c in range(x // 128, y // 128):
            m = mm(T.PV[:, c:c + 1], T.G[:, 128 * c:128 * c + 128], T.SEL[:, 0:1], True, True)
    need("v", m)
    ps = cp(T.PS[:, 0:8 * nq], T.PV[:, 0:8 * nq])

    tab_tok = []

    def tab_pass(lo, hi):
        for c in range(lo, hi):
            need("p", tab_tok[c])
            blk = T.TAB[:, c * CW:c * CW + CW]
            send([([own[oi + 1]], bits(topo.mask(core, own[oi + 1])), "ta%d" % c, blk, [blk])])

    if oi is not None:
        for c in range(NCH):
            tab_tok.append(("tl%d" % c, 16) if is_rank else expect("ta%d" % c, len(bits(topo.mask(own[oi - 1], core)))))
    if oi in (0, 1):
        tab_pass(0, BEFORE[oi])

    def served(c):
        return [own[o] for o in serve if own[o] != c]

    if served(core):
        need("p", ps)
        le = lookup_engines(topo, core, served(core))
        tr = []
        for k, o in enumerate(serve):
            d = own[o]
            if d != core:
                place = 16 * [c for c in mem if c != d].index(core)
                tr.append(([d], le[d], "pt_arr", T.PS[:, 16 * k:16 * k + 16], [T.PT[:, place:place + 16]]))
        send(tr)
    if oi in (0, 1):
        tab_pass(BEFORE[oi], NCH)

    if oi is not None:
        reqs = sets[oi]
        away = [cores[r] for r in reqs if cores[r] != core]
        T1, VV, PEN, FT = T.OW[:, 0:32], T.OW[:, 32:48], T.OW[:, 48:64], T.OW[:, 64:80]
        need("v", c_ml)
        c_lt = ts(T.LT[:], T.ML[:], T.PIX[:, 0:1], -1.0, OP.is_le, OP.mult)
        a = fill(T.RST[:], 1.0)
        need("v", a, c_e)
        for rr in range(2):
            fill(T.RST[:, 8 * rr:8 * rr + 1], 0.0)
        cp(T.REP[0:16, :], T.E[0:16, 0:128])
        ts(T.OX[:], T.LI[:, 0:16], -1.0, None, OP.add)
        if is_rank:
            fill(T.L[:, 0:CAPP], 0.0)
            for b in range(8):
                ts(T.EH[:, 128 * b:128 * b + 128], T.I128[:], T.P16[:, b:b + 1], None, OP.is_equal)
        gm, gs = [(gr[1], gr[2]) for gr in P["groups"] if gr[0] == si and oi in gr[2]][0]
        pt_n = sum(len(lookup_engines(topo, c, [own[o] for o in gs if own[o] != c])[core]) for c in gm if c != core)
        k = gs.index(oi)
        last = T.PS[:, 16 * k:16 * k + 16] if core in gm else T.PT[:, 48:64]
        need("v", ("cv", cnt["cv"]), expect("pt_arr", pt_n))
        tt(T1[:, 0:16], T.PT[:, 0:16], T.PT[:, 16:32], OP.add)
        a = tt(T1[:, 16:32], T.PT[:, 32:48], last, OP.add)
        need("v", a)
        a = tt(VV, T1[:, 0:16], T1[:, 16:32], OP.add)
        need("v", a)
        hit = ts(T.MM[:], VV, 0.5, None, OP.is_ge)
        need("v", hit)
        cum = did("v", g.vector.tensor_tensor_scan(T.CUM[:], T.RST[:], T.MM[:], 0.0, OP.mult, OP.add))
        ts(PEN, VV, 0.5, 4096.0, OP.is_lt, OP.mult)
        col = ts(T.COL[:], VV, -2049.0, None, OP.add)
        need("t", c_lt, hit)
        mm(T.PK[:, 0:16], T.LT[:], T.MM[:], True, False)
        need("t", cum)
        pk = mm(T.PK[:, 0:16], T.ONE[:, 0:128], T.CUM[:], False, True)
        need("v", pk, col)
        a = tt(T.KI[:], T.PK[:, 0:16], PEN, OP.add)
        need("s", a)
        ft = act(FT, T.PK[:, 0:16], 1.0, float(CAPP * (si + 1)))
        need("v", a)
        klo = ts(T.KLH[:, 0:16], T.KI[:], 15, None, OP.bitwise_and)
        khi = ts(T.KLH[:, 16:32], T.KI[:], 4, None, OP.logical_shift_right)
        land = T.L[:, CAPP * (si + 1):CAPP * (si + 2)]
        PLs, PRs = [T.PL, T.PX], [T.PQ0, T.PQ1]
        own_tok, lists, rows = [], {}, {}

        def half(buf, rr):
            return buf[:, 128 * rr:128 * rr + 128]

        def onehot_a(rr):
            need("v", klo, c_i128)
            return tt(half(T.AH, rr), T.KLH[:, 0:16].indirect(T.OX[:, 8 * rr:8 * rr + 8]), T.I128[:], OP.is_equal)

        def onehot_b(rr):
            need("v", khi)
            return tt(half(T.BQ, rr), T.KLH[:, 16:32].indirect(T.OX[:, 8 * rr:8 * rr + 8]), T.I128[:], OP.is_equal)

        def onehot_c(rr, b):
            need("v", b)
            b = tt(half(T.BH, rr), T.COL[:].indirect(T.OX[:, 8 * rr:8 * rr + 8]), half(T.BQ, rr), OP.mult)
            need("t", b)
            for c in range(8):
                x = 128 * rr + 16 * c
                lists[rr] = mm(PLs[rr][0:16, 0:16], T.AH[:, x:x + 16], T.BH[:, x:x + 16], c == 0, c == 7)

        def spread_list(rr):
            need("v", lists[rr])
            a = cp(T.LS[0:16, 16 * rr:16 * rr + 16], PLs[rr][0:16, 0:16])
            need("t", a)
            rows[rr] = mm(PRs[rr][:, 0:16], T.REP[0:16, :], T.LS[0:16, 16 * rr:16 * rr + 16], True, True)

        def deliver(rr, q):
            r = reqs[rr]
            need("v", rows[rr])
            lst = ts(T.LST[:, 16 * rr:16 * rr + 16], PRs[rr][:, 0:16], 2048.0, None, OP.add)
            need(q, lst, *tab_tok)
            here = cores[r] == core
            out = land if here else T.DT[:, CAPP * rr:CAPP * rr + CAPP]
            src = T.TAB[:].indirect(T.LST[:, 16 * rr:16 * rr + 16])
            d = act(out, src) if q == "s" else cp(out, src)
            if here:
                own_tok.append(d)
            else:
                need("p", d)
                send([([cores[r]], bits(topo.mask(core, cores[r])), "dt_arr", out, [land])])

        onehot_a(0)
        onehot_c(0, onehot_b(0))
        need("v", ft)
        for rr, r in enumerate(reqs):
            out = T.SL[:, 8 * si:8 * si + 8] if cores[r] == core else T.F[:, 8 * rr:8 * rr + 8]
            ff = tt(out, FT[:, 8 * rr:8 * rr + 8], T.MM[:, 8 * rr:8 * rr + 8], OP.mult)
        need("p", ff)
        se = split_engines(topo, core, away, 4)
        send([([cores[r]], se[cores[r]], "sl_arr", T.F[:, 8 * rr:8 * rr + 8], [T.SL[:, 8 * si:8 * si + 8]])
              for rr, r in enumerate(reqs) if cores[r] != core])
        spread_list(0)
        onehot_a(1)
        b1 = onehot_b(1)
        deliver(0, "s")
        onehot_c(1, b1)
        spread_list(1)
        deliver(1, "v")

    if is_rank:
        sl_n = dt_n = 0
        for tm in P["teams"]:
            for src, q in zip(tm["own"], tm["sets"]):
                if si in q and src != core:
                    to = [cores[r] for r in q if cores[r] != src]
                    sl_n += len(split_engines(topo, src, to, 4)[core])
                    dt_n += len(bits(topo.mask(src, core)))
        need("v", expect("sl_arr", sl_n), ("cv", cnt["cv"]))
        a = tt(T.SA[:, 0:24], T.SL[:, 0:24], T.SL[:, 24:48], OP.add)
        need("v", a)
        a = tt(T.SA[:, 24:32], T.SA[:, 0:8], T.SA[:, 8:16], OP.add)
        need("v", a)
        a = tt(T.SA[:, 32:40], T.SA[:, 24:32], T.SA[:, 16:24], OP.add)
        need("t", a)
        for b in range(8):
            m = mm(T.PW[:, b:64:8], T.EH[:, 128 * b:128 * b + 128], T.SA[:, 32:40], True, True)
        need("v", m)
        a = cp(T.SLU[:], T.PW[:, 0:64])
        dta = expect("dt_arr", dt_n)
        need("v", a, dta, *own_tok)
        need("s", a, dta, *own_tok)
        v = [cp(T.YT[:, x:x + 256], T.L[:].indirect(T.SLU[:, x // 16:x // 16 + 16])) for x in (0, 256)]
        w = [act(T.YT[:, x:x + 256], T.L[:].indirect(T.SLU[:, x // 16:x // 16 + 16])) for x in (512, 768)]
        for q, tok, x in (("y", v[0], 0), ("y", w[0], 512), ("y", v[1], 256), ("s", w[1], 768)):
            need(q, tok)
            dma(q, "st", T.y[:, x:x + 256], T.YT[:, x:x + 256])

    for sem in tot:
        need("p", (sem, tot[sem]))
    for sem in cnt:
        if cnt[sem]:
            need("p", (sem, cnt[sem]))
